import numpy as np
import ml_dtypes


def mxq(x, axis, fmt="e4m3"):
    dtype, down = {"e4m3": (ml_dtypes.float8_e4m3fn, 7), "e5m2": (ml_dtypes.float8_e5m2, 14)}[fmt]
    v = np.moveaxis(np.asarray(x, np.float32).astype(ml_dtypes.bfloat16).astype(np.float64), axis, -1)
    blocks = v.reshape(v.shape[:-1] + (-1, 32))
    amax = np.abs(blocks).max(-1, keepdims=True)
    byte = np.maximum(np.where(amax > 0, np.frexp(amax)[1] - 1 + 127, 0) - down, 1)
    scale = np.exp2(byte - 127.0)
    codes = (blocks / scale).astype(np.float32).astype(dtype).astype(np.float64)
    return np.moveaxis((codes * scale).reshape(v.shape), -1, axis)


WIDE = False


def mx_kscale(k):
    if not WIDE:
        return np.ones(k)
    levels = np.array([10, -10, 5, -5, 0])
    if k % 512:
        return np.exp2(np.random.permutation(np.resize(levels, k // 32))).repeat(32)
    a = np.empty((k // 512, 16))
    for p in range(k // 512):
        a[p, :8] = np.random.permutation(np.resize(levels, 8))
        for g in range(8):
            far = levels[np.abs(levels - a[p, g]) >= 10]
            a[p, g + 8] = far[np.random.randint(len(far))]
    return np.exp2(a.ravel()).repeat(32)


def f64(x):
    return np.asarray(x).astype(np.float64)


def striped(idx):
    return np.tile(idx.reshape(-1, 16).T, (8, 1)).astype(np.uint16)


def unstriped(offs):
    return offs[:16].T.reshape(-1).astype(np.int64)


def striped8(idx):
    return np.concatenate([x.reshape(-1, 16).T for x in idx]).astype(np.uint16)


def runs(offs, k):
    lists = np.stack([offs[16 * r : 16 * r + 16].T.reshape(-1) for r in range(8)]).astype(np.int64)
    return lists[np.arange(k) % 512 // 64]


def pack_weight(w):
    k, n = w.shape
    w = f64(np.asarray(w, np.float32).astype(ml_dtypes.bfloat16)).reshape(k // 32, 32, n)
    amax = np.abs(w).max(1)
    byte = np.clip(np.where(amax > 0, np.frexp(amax)[1] - 1 + 127 - 7, 1), 1, 254)
    scaled = (w * np.exp2(127.0 - byte)[:, None, :]).reshape(k, n).astype(np.float32)
    words = np.ascontiguousarray(scaled.reshape(k // 512, 128, 4, n).transpose(0, 1, 3, 2)).astype(ml_dtypes.float8_e4m3fn).view(np.uint8)
    return words, np.ascontiguousarray(byte.astype(np.uint8).reshape(k // 512, 16, n))


def unpack_weight(words, scales):
    g, p, n, _ = words.shape
    vals = np.ascontiguousarray(words).view(ml_dtypes.float8_e4m3fn).astype(np.float64) * np.repeat(np.exp2(scales.astype(np.float64) - 127.0), 8, axis=1)[..., None]
    return vals.transpose(0, 1, 3, 2).reshape(g * 512, n)

def planes(y):
    n, m = y.shape
    v = y.astype(np.float32).astype(ml_dtypes.bfloat16).astype(np.float64).reshape(n // 32, 32, m)
    top = np.abs(v).max(1)
    byte = np.clip(np.where(top > 0, np.frexp(top)[1] - 1 + 127 - 7, 1), 1, 254)
    codes = (v * np.exp2(127.0 - byte)[:, None, :]).reshape(n, m).astype(np.float32).astype(ml_dtypes.float8_e4m3fn).view(np.uint8)
    words = codes.reshape(n // 512, 128, 4, m).transpose(0, 1, 3, 2)
    return np.ascontiguousarray(words), np.ascontiguousarray(byte.astype(np.uint8).reshape(n // 512, 16, m))


K, T, S, V, N, H = 512, 2048, 512, 512, 512, 512


def setup_inputs():
    n = np.random.standard_normal
    s = mx_kscale(K)[:, None]
    u = mx_kscale(H)
    packed_xT = pack_weight(n((K, T)) * s)
    packed_w3 = pack_weight(n((H, N)) / np.sqrt(2 * H) / u[:, None])
    packed_w4 = pack_weight(n((H, N)) / np.sqrt(2 * H) / u[:, None])
    return {
        "x_words": packed_xT[0],
        "x_scales": packed_xT[1],
        "w1": (n((K, H)) / np.sqrt(K) / s * u).astype(np.float32),
        "w2": (n((K, H)) / np.sqrt(K) / s * u).astype(np.float32),
        "w3_words": packed_w3[0],
        "w3_scales": packed_w3[1],
        "w4_words": packed_w4[0],
        "w4_scales": packed_w4[1],
        "offs": striped(np.random.permutation(T)[:S]),
        "book": striped(np.random.permutation(T)[:V]),
        "c1": striped8(np.random.randint(0, V, (8, S))),
        "c2": striped8(np.random.randint(0, V, (8, S))),
    }


def reference(x_words, x_scales, w1, w2, w3_words, w3_scales, w4_words, w4_scales, offs, book, c1, c2):
    xq = unpack_weight(x_words, x_scales)[:, unstriped(offs)]
    y = mxq(f64(w1), 0, "e4m3").T @ xq
    x_book = unpack_weight(x_words, x_scales)[:, unstriped(book)]
    c = mxq(f64(w2), 0, "e4m3").T @ x_book
    r1 = y - (c[np.arange(H)[:, None], runs(c1, H)])
    z = r1 - (0.5 * (c[np.arange(H)[:, None], runs(c2, H)]))
    out_0 = unpack_weight(w3_words, w3_scales).T @ mxq(r1, 0, "e4m3") + unpack_weight(w4_words, w4_scales).T @ mxq(z, 0, "e4m3")
    return (out_0,) + planes(out_0)

@@ -1,0 +1,249 @@
+from contextlib import ExitStack
+
+import concourse.mybir as mybir
+
+K, T, S, V, H, N = 512, 2048, 512, 512, 512, 512
+FLOPS = 2 * (K * H * S + K * H * V + 2 * H * N * S)
+
+F32 = mybir.dt.float32
+BF16 = mybir.dt.bfloat16
+I32 = mybir.dt.int32
+U32 = mybir.dt.uint32
+U16 = mybir.dt.uint16
+U8 = mybir.dt.uint8
+FP8X4 = mybir.dt.float8_e4m3fn_x4
+MULT = mybir.AluOpType.mult
+ADD = mybir.AluOpType.add
+COPY = mybir.ActivationFunctionType.Copy
+
+P = 128
+PACK = 4
+QUADS = 4
+QUARTER = 128
+HALF = 256
+CHUNKS = ((0, 256), (256, 128), (384, 128))
+
+
+def tile_picked_rvqres_none_po_kernel(
+    tc, x_words, x_scales, w1, w2, w3_words, w3_scales, w4_words, w4_scales, offs, book, c1, c2, out_0, out_1, out_2
+):
+    nc = tc.nc
+    with ExitStack() as ctx:
+        keep = ctx.enter_context(tc.tile_pool(name="keep", bufs=1))
+        psum = ctx.enter_context(tc.psum_pool(name="psum", bufs=1))
+
+        def new(name, shape, dtype):
+            return keep.tile(shape, dtype, name=name, align_bytes=64)
+
+        def bank(index, name, shape):
+            return psum.tile(shape, F32, name=name, tag="bank%d" % index)
+
+        def load_list(name, src):
+            tile = new(name, [P, S // 16], U16)
+            nc.sync.dma_start(tile[:], src)
+            return tile
+
+        def load_scale_rows(queue, tile, first_row, src):
+            for q in range(QUADS):
+                queue.dma_start(
+                    out=tile[32 * q + first_row : 32 * q + first_row + 4, :].bitcast(I32),
+                    in_=src[0, 4 * q : 4 * q + 4, :].bitcast(I32),
+                )
+
+        def words_of(src):
+            return src[0].rearrange("p n r -> p (n r)").bitcast(I32)
+
+        xs = new("xs", [P, T], U8)
+        nc.vector.memset(xs[:].bitcast(I32), 0)
+        ws = new("ws", [P, N], U8)
+        nc.vector.memset(ws[:].bitcast(I32), 0)
+        book_t = load_list("book_t", book)
+        offs_t = load_list("offs_t", offs)
+        raw = {}
+
+        def load_half(name, w, h):
+            raw[name, h] = new("%s_raw%d" % (name, h), [P, PACK, HALF], F32)
+            nc.sync.dma_start(
+                out=raw[name, h][:],
+                in_=w.rearrange("(p j) c -> p j c", j=PACK)[:, :, h * HALF : (h + 1) * HALF],
+            )
+
+        load_half("w2", w2, 0)
+        load_scale_rows(nc.sync, xs, 0, x_scales)
+        load_half("w2", w2, 1)
+        xw = new("xw", [P, T], I32)
+        nc.sync.dma_start(out=xw[:], in_=words_of(x_words))
+        load_half("w1", w1, 0)
+        load_half("w1", w1, 1)
+        c1_t = load_list("c1_t", c1)
+        c2_t = load_list("c2_t", c2)
+        ww = new("ww", [P, 2, N], I32)
+        nc.sync.dma_start(out=ww[:, 0, :], in_=words_of(w3_words))
+        nc.sync.dma_start(out=ww[:, 1, :], in_=words_of(w4_words))
+        load_scale_rows(nc.sync, ws, 0, w3_scales)
+        load_scale_rows(nc.sync, ws, 4, w4_scales)
+
+        bs = new("bs", [P, V], U8)
+        nc.vector.tensor_copy(bs[:], xs[:].indirect(book_t[:]))
+        ps = new("ps", [P, S], U8)
+        nc.vector.tensor_copy(ps[:], xs[:].indirect(offs_t[:]))
+
+        def dealt_views(grouped, name, h):
+            dst = grouped[:].rearrange("p (t m j) -> p m t j", t=PACK, j=PACK)[:, h * 64 : (h + 1) * 64]
+            src = raw[name, h][:].rearrange("p j (m t) -> p m t j", t=PACK)
+            return dst, src
+
+        def quantize(name, grouped, width):
+            codes = new(name + "_codes", [P, width], U32)
+            scales = new(name + "_scales", [P, width], U8)
+            nc.vector.quantize_mx(out=codes[:].bitcast(FP8X4), scales=scales[:], in_=grouped[:])
+            return codes, scales
+
+        def mm(out, lhs_codes, lhs_scales, rhs_codes, rhs_scales, start=True, stop=True):
+            nc.tensor.matmul_mx(
+                out=out, lhsT=lhs_codes.bitcast(FP8X4), lhsT_scale=lhs_scales,
+                rhs=rhs_codes.bitcast(FP8X4), rhs_scale=rhs_scales, start=start, stop=stop,
+            )
+
+        w2_bf = new("w2_bf", [P, H * PACK], BF16)
+        for h in range(2):
+            dst, src = dealt_views(w2_bf, "w2", h)
+            nc.scalar.activation(dst, src, COPY)
+        w2_codes, w2_sc = quantize("w2", w2_bf, H)
+        bw = new("bw", [P, V], U32)
+        nc.vector.tensor_copy(bw[:], xw[:].bitcast(U32).indirect(book_t[:]))
+        pw = new("pw", [P, S], U32)
+        nc.vector.tensor_copy(pw[:], xw[:].bitcast(U32).indirect(offs_t[:]))
+        c_acc = []
+        for t in range(PACK):
+            cols = slice(t * P, (t + 1) * P)
+            c_acc.append(bank(t, "c_acc%d" % t, [P, V]))
+            mm(c_acc[t][:], w2_codes[:, cols], w2_sc[:, cols], bw[:], bs[:])
+        windows = [new("window%d" % t, [P, V], F32) for t in range(PACK)]
+        g1 = [new("g1_%d" % h, [P, PACK, HALF], F32) for h in range(2)]
+        w1_bf = new("w1_bf", [P, H * PACK], BF16)
+
+        def first_lookup(t):
+            nc.scalar.activation(windows[t][:], c_acc[t][:], COPY, scale=-0.5)
+            for h in range(2):
+                nc.vector.tensor_copy(g1[h][:, t, :], windows[t][:].indirect(c1_t[:, 16 * h : 16 * (h + 1)]))
+
+        def cast_w1(h):
+            dst, src = dealt_views(w1_bf, "w1", h)
+            for a in range(0, 64, 32):
+                nc.scalar.copy(dst[:, a : a + 32], src[:, a : a + 32])
+
+        first_lookup(0)
+        first_lookup(1)
+        cast_w1(0)
+        first_lookup(2)
+        cast_w1(1)
+        w1_codes, w1_sc = quantize("w1", w1_bf, H)
+        first_lookup(3)
+        y = []
+        for q in range(S // QUARTER):
+            acc = bank(4 + q, "y_acc%d" % q, [P, PACK, QUARTER])
+            js = slice(q * QUARTER, (q + 1) * QUARTER)
+            for t in range(PACK):
+                cols = slice(t * P, (t + 1) * P)
+                mm(acc[:, t, :], w1_codes[:, cols], w1_sc[:, cols], pw[:, js], ps[:, js])
+            y.append(acc)
+
+        wd = new("wd", [P, 2, N], I32)
+        nc.vector.tensor_copy(
+            wd[:].rearrange("p w (t a b) -> p w a t b", t=PACK, b=4),
+            ww[:].rearrange("p w (a b t) -> p w a t b", t=PACK, b=4),
+        )
+        wsd = new("wsd", [P, N], U8)
+        nc.vector.tensor_copy(
+            wsd[:].rearrange("p (t a b) -> p a t b", t=PACK, b=16),
+            ws[:].rearrange("p (a b t) -> p a t b", t=PACK, b=16),
+        )
+
+        out_codes = new("out_codes", [P, S], I32)
+        out_scales = new("out_scales", [P, S], U8)
+        out_rows = out_0.rearrange("(p t) j -> p t j", t=PACK)
+        out_words = words_of(out_1)
+
+        def interleave(name, src, width):
+            grouped = new(name, [P, width * PACK], BF16)
+            nc.scalar.copy(
+                grouped[:].rearrange("p (c i t) -> p c t i", i=4, t=PACK),
+                src[:].rearrange("p t (c i) -> p c t i", i=4),
+            )
+            return grouped
+
+        r1, r1_bf, z_bf, r1_q, z_q = {}, {}, {}, {}, {}
+
+        def first_residual(n):
+            start, width = CHUNKS[n]
+            r1[n] = new("r1_%d" % n, [P, PACK, width], F32)
+            for a in range(0, width, QUARTER):
+                j = start + a
+                nc.vector.scalar_tensor_tensor(
+                    r1[n][:, :, a : a + QUARTER], g1[j // HALF][:, :, j % HALF : j % HALF + QUARTER], 2.0,
+                    y[j // QUARTER][:], MULT, ADD,
+                )
+            r1_bf[n] = interleave("r1_bf%d" % n, r1[n], width)
+
+        def second_residual(n):
+            start, width = CHUNKS[n]
+            z = new("z_%d" % n, [P, PACK, width], F32)
+            lst = c2_t[:, start // 16 : (start + width) // 16]
+            for t in range(PACK):
+                nc.vector.tensor_tensor(z[:, t, :], windows[t][:].indirect(lst), r1[n][:, t, :], ADD)
+            z_bf[n] = interleave("z_bf%d" % n, z, width)
+
+        out_bf = {}
+
+        def product(n):
+            start, width = CHUNKS[n]
+            for a in range(0, width, QUARTER):
+                q = (start + a) // QUARTER
+                js = slice(a, a + QUARTER)
+                acc = bank(q, "out_acc%d" % q, [P, PACK, QUARTER])
+                for t in range(PACK):
+                    cols = slice(t * P, (t + 1) * P)
+                    mm(acc[:, t, :], wd[:, 0, cols], wsd[:, cols], r1_q[n][0][:, js], r1_q[n][1][:, js], True, False)
+                    mm(acc[:, t, :], wd[:, 1, cols], wsd[4:P, cols], z_q[n][0][:, js], z_q[n][1][:, js], False, True)
+                out_bf[q] = new("out_bf%d" % q, [P, QUARTER * PACK], BF16)
+                dst = out_bf[q][:].rearrange("p (n t) -> p n t", t=PACK)
+                src = acc[:].rearrange("p t n -> p n t")
+                if q == S // QUARTER - 1:
+                    nc.vector.tensor_copy(dst, src)
+                else:
+                    nc.scalar.copy(dst, src)
+                res = new("res%d" % q, [P, PACK, QUARTER], F32)
+                nc.scalar.copy(res[:], acc[:])
+                nc.sync.dma_start(out=out_rows[:, :, q * QUARTER : (q + 1) * QUARTER], in_=res[:])
+
+        def planes(q):
+            js = slice(q * QUARTER, (q + 1) * QUARTER)
+            nc.vector.quantize_mx(out=out_codes[:, js].bitcast(FP8X4), scales=out_scales[:, js], in_=out_bf[q][:])
+            nc.sync.dma_start(out=out_words[:, js], in_=out_codes[:, js])
+
+        first_residual(0)
+        first_residual(1)
+        first_residual(2)
+        second_residual(0)
+        r1_q[0] = quantize("r1_0", r1_bf[0], 256)
+        r1_q[1] = quantize("r1_1", r1_bf[1], 128)
+        second_residual(1)
+        r1_q[2] = quantize("r1_2", r1_bf[2], 128)
+        z_q[0] = quantize("z_0", z_bf[0], 256)
+        product(0)
+        second_residual(2)
+        z_q[1] = quantize("z_1", z_bf[1], 128)
+        product(1)
+        planes(0)
+        planes(1)
+        z_q[2] = quantize("z_2", z_bf[2], 128)
+        product(2)
+        planes(2)
+        planes(3)
+        for q in range(QUADS):
+            queue = nc.sync if q % 2 else nc.scalar
+            queue.dma_start(
+                out=out_2[0, 4 * q : 4 * q + 4, :].bitcast(I32),
+                in_=out_scales[32 * q : 32 * q + 4, :].bitcast(I32),
+            )

@@ -21,7 +21,7 @@ PACK = 4
 QUADS = 4
 QUARTER = 128
 HALF = 256
-CHUNKS = ((0, 256), (256, 128), (384, 128))
+CHUNKS = ((0, 128), (128, 128), (256, 128), (384, 128))
 
 
 def tile_picked_rvqres_none_po_kernel(
@@ -73,9 +73,9 @@ def tile_picked_rvqres_none_po_kernel(
         load_half("w2", w2, 1)
         xw = new("xw", [P, T], I32)
         nc.sync.dma_start(out=xw[:], in_=words_of(x_words))
+        c1_t = load_list("c1_t", c1)
         load_half("w1", w1, 0)
         load_half("w1", w1, 1)
-        c1_t = load_list("c1_t", c1)
         c2_t = load_list("c2_t", c2)
         ww = new("ww", [P, 2, N], I32)
         nc.sync.dma_start(out=ww[:, 0, :], in_=words_of(w3_words))
@@ -111,20 +111,29 @@ def tile_picked_rvqres_none_po_kernel(
             nc.scalar.activation(dst, src, COPY)
         w2_codes, w2_sc = quantize("w2", w2_bf, H)
         bw = new("bw", [P, V], U32)
-        nc.vector.tensor_copy(bw[:], xw[:].bitcast(U32).indirect(book_t[:]))
+        for h in range(2):
+            nc.vector.tensor_copy(
+                bw[:, h * HALF : (h + 1) * HALF], xw[:].bitcast(U32).indirect(book_t[:, 16 * h : 16 * (h + 1)])
+            )
         pw = new("pw", [P, S], U32)
         nc.vector.tensor_copy(pw[:], xw[:].bitcast(U32).indirect(offs_t[:]))
-        c_acc = []
+        c_parts = []
         for t in range(PACK):
             cols = slice(t * P, (t + 1) * P)
-            c_acc.append(bank(t, "c_acc%d" % t, [P, V]))
-            mm(c_acc[t][:], w2_codes[:, cols], w2_sc[:, cols], bw[:], bs[:])
+            spans = ((0, HALF, 4), (HALF, V, 0)) if t == 0 else ((0, V, t),)
+            parts = []
+            for lo, hi, b in spans:
+                acc = bank(b, "c_acc%d_%d" % (t, lo), [P, hi - lo])
+                mm(acc[:], w2_codes[:, cols], w2_sc[:, cols], bw[:, lo:hi], bs[:, lo:hi])
+                parts.append((lo, hi, acc))
+            c_parts.append(parts)
         windows = [new("window%d" % t, [P, V], F32) for t in range(PACK)]
         g1 = [new("g1_%d" % h, [P, PACK, HALF], F32) for h in range(2)]
         w1_bf = new("w1_bf", [P, H * PACK], BF16)
 
         def first_lookup(t):
-            nc.scalar.activation(windows[t][:], c_acc[t][:], COPY, scale=-0.5)
+            for lo, hi, acc in c_parts[t]:
+                nc.scalar.activation(windows[t][:, lo:hi], acc[:], COPY, scale=-0.5)
             for h in range(2):
                 nc.vector.tensor_copy(g1[h][:, t, :], windows[t][:].indirect(c1_t[:, 16 * h : 16 * (h + 1)]))
 
@@ -150,14 +159,15 @@ def tile_picked_rvqres_none_po_kernel(
             y.append(acc)
 
         wd = new("wd", [P, 2, N], I32)
-        nc.vector.tensor_copy(
-            wd[:].rearrange("p w (t a b) -> p w a t b", t=PACK, b=4),
-            ww[:].rearrange("p w (a b t) -> p w a t b", t=PACK, b=4),
-        )
+        for w in range(2):
+            nc.gpsimd.tensor_copy(
+                wd[:, w, :].rearrange("p (t m) -> p t m", t=PACK),
+                ww[:, w, :].rearrange("p (m t) -> p t m", t=PACK),
+            )
         wsd = new("wsd", [P, N], U8)
-        nc.vector.tensor_copy(
-            wsd[:].rearrange("p (t a b) -> p a t b", t=PACK, b=16),
-            ws[:].rearrange("p (a b t) -> p a t b", t=PACK, b=16),
+        nc.gpsimd.tensor_copy(
+            wsd[:].rearrange("p (t m) -> p t m", t=PACK),
+            ws[:].rearrange("p (m t) -> p t m", t=PACK),
         )
 
         out_codes = new("out_codes", [P, S], I32)
@@ -165,13 +175,23 @@ def tile_picked_rvqres_none_po_kernel(
         out_rows = out_0.rearrange("(p t) j -> p t j", t=PACK)
         out_words = words_of(out_1)
 
-        def interleave(name, src, width):
-            grouped = new(name, [P, width * PACK], BF16)
-            nc.scalar.copy(
-                grouped[:].rearrange("p (c i t) -> p c t i", i=4, t=PACK),
-                src[:].rearrange("p t (c i) -> p c t i", i=4),
+        rz_bf = [new("rz_bf%d" % q, [P, 2, QUARTER * PACK], BF16) for q in range(4)]
+        rz_codes = [new("rz_codes%d" % q, [P, 2, QUARTER], U32) for q in range(4)]
+        rz_scales = [new("rz_scales%d" % q, [P, 2, QUARTER], U8) for q in range(4)]
+
+        def interleave(grouped, src, step=PACK):
+            for t in range(0, PACK, step):
+                nc.scalar.copy(
+                    grouped.rearrange("p (c i t) -> p c t i", i=4, t=PACK)[:, :, t : t + step, :],
+                    src[:].rearrange("p t (c i) -> p c t i", i=4)[:, :, t : t + step, :],
+                )
+
+        def quantize_residuals(q, which):
+            nc.vector.quantize_mx(
+                out=rz_codes[q][:, which, :].rearrange("p a n -> p (a n)").bitcast(FP8X4),
+                scales=rz_scales[q][:, which, :].rearrange("p a n -> p (a n)"),
+                in_=rz_bf[q][:, which, :].rearrange("p a n -> p (a n)"),
             )
-            return grouped
 
         r1, r1_bf, z_bf, r1_q, z_q = {}, {}, {}, {}, {}
 
@@ -184,7 +204,7 @@ def tile_picked_rvqres_none_po_kernel(
                     r1[n][:, :, a : a + QUARTER], g1[j // HALF][:, :, j % HALF : j % HALF + QUARTER], 2.0,
                     y[j // QUARTER][:], MULT, ADD,
                 )
-            r1_bf[n] = interleave("r1_bf%d" % n, r1[n], width)
+            interleave(rz_bf[n][:, 0, :], r1[n])
 
         def second_residual(n):
             start, width = CHUNKS[n]
@@ -192,55 +212,55 @@ def tile_picked_rvqres_none_po_kernel(
             lst = c2_t[:, start // 16 : (start + width) // 16]
             for t in range(PACK):
                 nc.vector.tensor_tensor(z[:, t, :], windows[t][:].indirect(lst), r1[n][:, t, :], ADD)
-            z_bf[n] = interleave("z_bf%d" % n, z, width)
+            interleave(rz_bf[n][:, 1, :], z, 2 if n == 3 else PACK)
 
-        out_bf = {}
 
-        def product(n):
-            start, width = CHUNKS[n]
-            for a in range(0, width, QUARTER):
-                q = (start + a) // QUARTER
-                js = slice(a, a + QUARTER)
-                acc = bank(q, "out_acc%d" % q, [P, PACK, QUARTER])
-                for t in range(PACK):
-                    cols = slice(t * P, (t + 1) * P)
-                    mm(acc[:, t, :], wd[:, 0, cols], wsd[:, cols], r1_q[n][0][:, js], r1_q[n][1][:, js], True, False)
-                    mm(acc[:, t, :], wd[:, 1, cols], wsd[4:P, cols], z_q[n][0][:, js], z_q[n][1][:, js], False, True)
-                out_bf[q] = new("out_bf%d" % q, [P, QUARTER * PACK], BF16)
-                dst = out_bf[q][:].rearrange("p (n t) -> p n t", t=PACK)
-                src = acc[:].rearrange("p t n -> p n t")
-                if q == S // QUARTER - 1:
-                    nc.vector.tensor_copy(dst, src)
-                else:
-                    nc.scalar.copy(dst, src)
-                res = new("res%d" % q, [P, PACK, QUARTER], F32)
-                nc.scalar.copy(res[:], acc[:])
-                nc.sync.dma_start(out=out_rows[:, :, q * QUARTER : (q + 1) * QUARTER], in_=res[:])
+        out_acc = {}
 
-        def planes(q):
-            js = slice(q * QUARTER, (q + 1) * QUARTER)
-            nc.vector.quantize_mx(out=out_codes[:, js].bitcast(FP8X4), scales=out_scales[:, js], in_=out_bf[q][:])
+        def product(q):
+            acc = bank(q, "out_acc%d" % q, [P, PACK, QUARTER])
+            for t in range(PACK):
+                cols = slice(t * P, (t + 1) * P)
+                mm(acc[:, t, :], wd[:, 0, cols], wsd[:, cols], rz_codes[q][:, 0, :], rz_scales[q][:, 0, :], True, False)
+                mm(acc[:, t, :], wd[:, 1, cols], wsd[4:P, cols], rz_codes[q][:, 1, :], rz_scales[q][:, 1, :], False, True)
+            out_acc[q] = acc
+
+        out_bf = new("out_bf", [P, S * PACK], BF16)
+        res = {}
+
+        def store(q):
+            res[q] = new("res%d" % q, [P, PACK, QUARTER], F32)
+            nc.scalar.copy(res[q][:], out_acc[q][:])
+            nc.sync.dma_start(out=out_rows[:, :, q * QUARTER : (q + 1) * QUARTER], in_=res[q][:])
+            nc.vector.tensor_copy(
+                out_bf[:, q * QUARTER * PACK : (q + 1) * QUARTER * PACK].rearrange("p (c i t) -> p c t i", i=4, t=PACK),
+                res[q][:].rearrange("p t (c i) -> p c t i", i=4),
+            )
+
+        def planes(h):
+            js = slice(h * HALF, (h + 1) * HALF)
+            nc.vector.quantize_mx(
+                out=out_codes[:, js].bitcast(FP8X4), scales=out_scales[:, js],
+                in_=out_bf[:, h * HALF * PACK : (h + 1) * HALF * PACK],
+            )
             nc.sync.dma_start(out=out_words[:, js], in_=out_codes[:, js])
 
         first_residual(0)
-        first_residual(1)
-        first_residual(2)
-        second_residual(0)
-        r1_q[0] = quantize("r1_0", r1_bf[0], 256)
-        r1_q[1] = quantize("r1_1", r1_bf[1], 128)
-        second_residual(1)
-        r1_q[2] = quantize("r1_2", r1_bf[2], 128)
-        z_q[0] = quantize("z_0", z_bf[0], 256)
-        product(0)
-        second_residual(2)
-        z_q[1] = quantize("z_1", z_bf[1], 128)
-        product(1)
+        for q in range(4):
+            if q < 3:
+                first_residual(q + 1)
+            if q > 0:
+                quantize_residuals(q - 1, slice(0, 2))
+                product(q - 1)
+                store(q - 1)
+            if q == 3:
+                quantize_residuals(q, slice(0, 1))
+            second_residual(q)
+        quantize_residuals(3, slice(1, 2))
+        product(3)
+        store(3)
         planes(0)
         planes(1)
-        z_q[2] = quantize("z_2", z_bf[2], 128)
-        product(2)
-        planes(2)
-        planes(3)
         for q in range(QUADS):
             queue = nc.sync if q % 2 else nc.scalar
             queue.dma_start(

@@ -21,7 +21,7 @@ PACK = 4
 QUADS = 4
 QUARTER = 128
 HALF = 256
-CHUNKS = ((0, 128), (128, 128), (256, 128), (384, 128))
+LAST = 3
 
 
 def tile_picked_rvqres_none_po_kernel(
@@ -30,10 +30,11 @@ def tile_picked_rvqres_none_po_kernel(
     nc = tc.nc
     with ExitStack() as ctx:
         keep = ctx.enter_context(tc.tile_pool(name="keep", bufs=1))
+        reused = ctx.enter_context(tc.tile_pool(name="reused", bufs=1))
         psum = ctx.enter_context(tc.psum_pool(name="psum", bufs=1))
 
-        def new(name, shape, dtype):
-            return keep.tile(shape, dtype, name=name, align_bytes=64)
+        def new(name, shape, dtype, tag=None):
+            return keep.tile(shape, dtype, name=name, tag=tag or name, align_bytes=64)
 
         def bank(index, name, shape):
             return psum.tile(shape, F32, name=name, tag="bank%d" % index)
@@ -53,10 +54,28 @@ def tile_picked_rvqres_none_po_kernel(
         def words_of(src):
             return src[0].rearrange("p n r -> p (n r)").bitcast(I32)
 
+        def entries(tile, start, count):
+            return tile[:, start // 16 : (start + count) // 16]
+
+        def quantize(codes, scales, grouped):
+            nc.vector.quantize_mx(out=codes.bitcast(FP8X4), scales=scales, in_=grouped)
+
+        def mm(out, lhs_codes, lhs_scales, rhs_codes, rhs_scales, start=True, stop=True):
+            nc.tensor.matmul_mx(
+                out=out, lhsT=lhs_codes.bitcast(FP8X4), lhsT_scale=lhs_scales,
+                rhs=rhs_codes.bitcast(FP8X4), rhs_scale=rhs_scales, start=start, stop=stop,
+            )
+
+        def woven(grouped, planes):
+            return (
+                grouped.rearrange("p (c i t) -> p c t i", i=4, t=PACK),
+                planes.rearrange("p t (c i) -> p c t i", i=4),
+            )
+
         xs = new("xs", [P, T], U8)
         nc.vector.memset(xs[:].bitcast(I32), 0)
         ws = new("ws", [P, N], U8)
-        nc.vector.memset(ws[:].bitcast(I32), 0)
+        nc.gpsimd.memset(ws[:].bitcast(I32), 0)
         book_t = load_list("book_t", book)
         offs_t = load_list("offs_t", offs)
         raw = {}
@@ -74,14 +93,14 @@ def tile_picked_rvqres_none_po_kernel(
         xw = new("xw", [P, T], I32)
         nc.sync.dma_start(out=xw[:], in_=words_of(x_words))
         c1_t = load_list("c1_t", c1)
+        load_scale_rows(nc.sync, ws, 0, w3_scales)
         load_half("w1", w1, 0)
         load_half("w1", w1, 1)
+        load_scale_rows(nc.sync, ws, 4, w4_scales)
         c2_t = load_list("c2_t", c2)
         ww = new("ww", [P, 2, N], I32)
         nc.sync.dma_start(out=ww[:, 0, :], in_=words_of(w3_words))
         nc.sync.dma_start(out=ww[:, 1, :], in_=words_of(w4_words))
-        load_scale_rows(nc.sync, ws, 0, w3_scales)
-        load_scale_rows(nc.sync, ws, 4, w4_scales)
 
         bs = new("bs", [P, V], U8)
         nc.vector.tensor_copy(bs[:], xs[:].indirect(book_t[:]))
@@ -93,27 +112,16 @@ def tile_picked_rvqres_none_po_kernel(
             src = raw[name, h][:].rearrange("p j (m t) -> p m t j", t=PACK)
             return dst, src
 
-        def quantize(name, grouped, width):
-            codes = new(name + "_codes", [P, width], U32)
-            scales = new(name + "_scales", [P, width], U8)
-            nc.vector.quantize_mx(out=codes[:].bitcast(FP8X4), scales=scales[:], in_=grouped[:])
-            return codes, scales
-
-        def mm(out, lhs_codes, lhs_scales, rhs_codes, rhs_scales, start=True, stop=True):
-            nc.tensor.matmul_mx(
-                out=out, lhsT=lhs_codes.bitcast(FP8X4), lhsT_scale=lhs_scales,
-                rhs=rhs_codes.bitcast(FP8X4), rhs_scale=rhs_scales, start=start, stop=stop,
-            )
-
         w2_bf = new("w2_bf", [P, H * PACK], BF16)
         for h in range(2):
-            dst, src = dealt_views(w2_bf, "w2", h)
-            nc.scalar.activation(dst, src, COPY)
-        w2_codes, w2_sc = quantize("w2", w2_bf, H)
+            nc.scalar.activation(*dealt_views(w2_bf, "w2", h), COPY)
+        w2_codes = new("w2_codes", [P, H], U32)
+        w2_sc = new("w2_sc", [P, H], U8)
+        quantize(w2_codes[:], w2_sc[:], w2_bf[:])
         bw = new("bw", [P, V], U32)
         for h in range(2):
             nc.vector.tensor_copy(
-                bw[:, h * HALF : (h + 1) * HALF], xw[:].bitcast(U32).indirect(book_t[:, 16 * h : 16 * (h + 1)])
+                bw[:, h * HALF : (h + 1) * HALF], xw[:].bitcast(U32).indirect(entries(book_t, h * HALF, HALF))
             )
         pw = new("pw", [P, S], U32)
         nc.vector.tensor_copy(pw[:], xw[:].bitcast(U32).indirect(offs_t[:]))
@@ -128,29 +136,29 @@ def tile_picked_rvqres_none_po_kernel(
                 parts.append((lo, hi, acc))
             c_parts.append(parts)
         windows = [new("window%d" % t, [P, V], F32) for t in range(PACK)]
-        g1 = [new("g1_%d" % h, [P, PACK, HALF], F32) for h in range(2)]
-        w1_bf = new("w1_bf", [P, H * PACK], BF16)
+        g1_halves = [new("g1_first", [P, PACK, HALF], F32)]
+        w1_bf = reused.tile([P, H * PACK], BF16, name="w1_bf", offset=2048, align_bytes=64)
 
-        def first_lookup(t):
+        def first_lookup(h, t):
+            nc.vector.tensor_copy(g1_halves[h][:, t, :], windows[t][:].indirect(entries(c1_t, h * HALF, HALF)))
+
+        for t in range(PACK):
             for lo, hi, acc in c_parts[t]:
                 nc.scalar.activation(windows[t][:, lo:hi], acc[:], COPY, scale=-0.5)
-            for h in range(2):
-                nc.vector.tensor_copy(g1[h][:, t, :], windows[t][:].indirect(c1_t[:, 16 * h : 16 * (h + 1)]))
-
-        def cast_w1(h):
+            first_lookup(0, t)
+        for h in range(2):
             dst, src = dealt_views(w1_bf, "w1", h)
             for a in range(0, 64, 32):
-                nc.scalar.copy(dst[:, a : a + 32], src[:, a : a + 32])
-
-        first_lookup(0)
-        first_lookup(1)
-        cast_w1(0)
-        first_lookup(2)
-        cast_w1(1)
-        w1_codes, w1_sc = quantize("w1", w1_bf, H)
-        first_lookup(3)
+                nc.gpsimd.tensor_copy(dst[:, a : a + 32], src[:, a : a + 32])
+        w1_codes = new("w1_codes", [P, H], U32)
+        w1_sc = new("w1_sc", [P, H], U8)
+        quantize(w1_codes[:], w1_sc[:], w1_bf[:])
+        g1_halves.append(reused.tile([P, PACK, HALF], F32, name="g1_second", offset=0, align_bytes=64))
+        for t in range(PACK):
+            first_lookup(1, t)
+        g1 = [g1_halves[q // 2][:, :, q % 2 * QUARTER : (q % 2 + 1) * QUARTER] for q in range(4)]
         y = []
-        for q in range(S // QUARTER):
+        for q in range(4):
             acc = bank(4 + q, "y_acc%d" % q, [P, PACK, QUARTER])
             js = slice(q * QUARTER, (q + 1) * QUARTER)
             for t in range(PACK):
@@ -158,11 +166,12 @@ def tile_picked_rvqres_none_po_kernel(
                 mm(acc[:, t, :], w1_codes[:, cols], w1_sc[:, cols], pw[:, js], ps[:, js])
             y.append(acc)
 
-        wd = new("wd", [P, 2, N], I32)
+        wd_both = reused.tile([P, 2, N], I32, name="wd_both", offset=4096, align_bytes=64)
+        wd = [wd_both[:, w, :] for w in range(2)]
         for w in range(2):
             nc.gpsimd.tensor_copy(
-                wd[:, w, :].rearrange("p (t m) -> p t m", t=PACK),
-                ww[:, w, :].rearrange("p (m t) -> p t m", t=PACK),
+                wd[w].rearrange("p (t c i) -> p c t i", t=PACK, i=4),
+                ww[:, w, :].rearrange("p (c i t) -> p c t i", t=PACK, i=4),
             )
         wsd = new("wsd", [P, N], U8)
         nc.gpsimd.tensor_copy(
@@ -174,93 +183,111 @@ def tile_picked_rvqres_none_po_kernel(
         out_scales = new("out_scales", [P, S], U8)
         out_rows = out_0.rearrange("(p t) j -> p t j", t=PACK)
         out_words = words_of(out_1)
+        out_bf = new("out_bf", [P, S * PACK], BF16)
 
         rz_bf = [new("rz_bf%d" % q, [P, 2, QUARTER * PACK], BF16) for q in range(4)]
         rz_codes = [new("rz_codes%d" % q, [P, 2, QUARTER], U32) for q in range(4)]
         rz_scales = [new("rz_scales%d" % q, [P, 2, QUARTER], U8) for q in range(4)]
 
-        def interleave(grouped, src, step=PACK):
-            for t in range(0, PACK, step):
-                nc.scalar.copy(
-                    grouped.rearrange("p (c i t) -> p c t i", i=4, t=PACK)[:, :, t : t + step, :],
-                    src[:].rearrange("p t (c i) -> p c t i", i=4)[:, :, t : t + step, :],
-                )
-
         def quantize_residuals(q, which):
-            nc.vector.quantize_mx(
-                out=rz_codes[q][:, which, :].rearrange("p a n -> p (a n)").bitcast(FP8X4),
-                scales=rz_scales[q][:, which, :].rearrange("p a n -> p (a n)"),
-                in_=rz_bf[q][:, which, :].rearrange("p a n -> p (a n)"),
+            quantize(
+                rz_codes[q][:, which, :].rearrange("p a n -> p (a n)"),
+                rz_scales[q][:, which, :].rearrange("p a n -> p (a n)"),
+                rz_bf[q][:, which, :].rearrange("p a n -> p (a n)"),
             )
 
-        r1, r1_bf, z_bf, r1_q, z_q = {}, {}, {}, {}, {}
+        r1 = {}
 
-        def first_residual(n):
-            start, width = CHUNKS[n]
-            r1[n] = new("r1_%d" % n, [P, PACK, width], F32)
-            for a in range(0, width, QUARTER):
-                j = start + a
-                nc.vector.scalar_tensor_tensor(
-                    r1[n][:, :, a : a + QUARTER], g1[j // HALF][:, :, j % HALF : j % HALF + QUARTER], 2.0,
-                    y[j // QUARTER][:], MULT, ADD,
-                )
-            interleave(rz_bf[n][:, 0, :], r1[n])
+        def first_residual(q, tag=None):
+            r1[q] = new("r1_%d" % q, [P, PACK, QUARTER], F32, tag)
+            nc.vector.scalar_tensor_tensor(r1[q][:], g1[q], 2.0, y[q][:], MULT, ADD)
+            nc.scalar.copy(*woven(rz_bf[q][:, 0, :], r1[q][:]))
 
-        def second_residual(n):
-            start, width = CHUNKS[n]
-            z = new("z_%d" % n, [P, PACK, width], F32)
-            lst = c2_t[:, start // 16 : (start + width) // 16]
+        def second_residual(q, tag=None):
+            z = new("z_%d" % q, [P, PACK, QUARTER], F32, tag)
             for t in range(PACK):
-                nc.vector.tensor_tensor(z[:, t, :], windows[t][:].indirect(lst), r1[n][:, t, :], ADD)
-            interleave(rz_bf[n][:, 1, :], z, 2 if n == 3 else PACK)
+                nc.vector.tensor_tensor(
+                    z[:, t, :], windows[t][:].indirect(entries(c2_t, q * QUARTER, QUARTER)), r1[q][:, t, :], ADD
+                )
+            dst, src = woven(rz_bf[q][:, 1, :], z[:])
+            step = 2 if q == LAST else PACK
+            for t in range(0, PACK, step):
+                nc.scalar.copy(dst[:, :, t : t + step], src[:, :, t : t + step])
 
+        def passes(acc, q, which, planes, start, stop):
+            for n, t in enumerate(planes):
+                cols = slice(t * P, (t + 1) * P)
+                mm(
+                    acc[:, n, :], wd[which][:, cols], wsd[4 * which : P, cols],
+                    rz_codes[q][:, which, :], rz_scales[q][:, which, :],
+                    start and n == 0, stop and n == len(planes) - 1,
+                )
+
+        def rounded(q):
+            return out_bf[:, q * QUARTER * PACK : (q + 1) * QUARTER * PACK]
 
         out_acc = {}
 
-        def product(q):
-            acc = bank(q, "out_acc%d" % q, [P, PACK, QUARTER])
-            for t in range(PACK):
-                cols = slice(t * P, (t + 1) * P)
-                mm(acc[:, t, :], wd[:, 0, cols], wsd[:, cols], rz_codes[q][:, 0, :], rz_scales[q][:, 0, :], True, False)
-                mm(acc[:, t, :], wd[:, 1, cols], wsd[4:P, cols], rz_codes[q][:, 1, :], rz_scales[q][:, 1, :], False, True)
-            out_acc[q] = acc
+        def open_product(q):
+            out_acc[q] = bank(q, "out_acc%d" % q, [P, PACK, QUARTER])
+            passes(out_acc[q], q, 0, range(PACK), True, False)
 
-        out_bf = new("out_bf", [P, S * PACK], BF16)
         res = {}
 
-        def store(q):
+        def close_product(q):
+            passes(out_acc[q], q, 1, range(PACK), False, True)
             res[q] = new("res%d" % q, [P, PACK, QUARTER], F32)
             nc.scalar.copy(res[q][:], out_acc[q][:])
             nc.sync.dma_start(out=out_rows[:, :, q * QUARTER : (q + 1) * QUARTER], in_=res[q][:])
-            nc.vector.tensor_copy(
-                out_bf[:, q * QUARTER * PACK : (q + 1) * QUARTER * PACK].rearrange("p (c i t) -> p c t i", i=4, t=PACK),
-                res[q][:].rearrange("p t (c i) -> p c t i", i=4),
-            )
 
-        def planes(h):
-            js = slice(h * HALF, (h + 1) * HALF)
-            nc.vector.quantize_mx(
-                out=out_codes[:, js].bitcast(FP8X4), scales=out_scales[:, js],
-                in_=out_bf[:, h * HALF * PACK : (h + 1) * HALF * PACK],
-            )
+        def planes(start, count):
+            js = slice(start, start + count)
+            quantize(out_codes[:, js], out_scales[:, js], out_bf[:, start * PACK : (start + count) * PACK])
             nc.sync.dma_start(out=out_words[:, js], in_=out_codes[:, js])
 
+        both, only_r1, only_z = slice(0, 2), slice(0, 1), slice(1, 2)
+
+        def finish(q):
+            quantize_residuals(q, both)
+            open_product(q)
+            close_product(q)
+            nc.vector.tensor_copy(*woven(rounded(q), res[q][:]))
+
         first_residual(0)
-        for q in range(4):
-            if q < 3:
-                first_residual(q + 1)
-            if q > 0:
-                quantize_residuals(q - 1, slice(0, 2))
-                product(q - 1)
-                store(q - 1)
-            if q == 3:
-                quantize_residuals(q, slice(0, 1))
-            second_residual(q)
-        quantize_residuals(3, slice(1, 2))
-        product(3)
-        store(3)
-        planes(0)
-        planes(1)
+        first_residual(1)
+        second_residual(0)
+        first_residual(2)
+        finish(0)
+        second_residual(1)
+        first_residual(3)
+        finish(1)
+        second_residual(2)
+        finish(2)
+        quantize_residuals(LAST, only_r1)
+        last_acc = [bank(3 + u, "last_acc%d" % u, [P, 2, QUARTER]) for u in range(2)]
+        for u in range(2):
+            passes(last_acc[u], LAST, 0, (2 * u, 2 * u + 1), True, False)
+        second_residual(LAST)
+        quantize_residuals(LAST, only_z)
+        for u in range(2):
+            passes(last_acc[u], LAST, 1, (2 * u, 2 * u + 1), False, True)
+        planes(0, HALF)
+        res_last = new("res_last", [P, PACK, QUARTER], F32)
+        js = slice(LAST * QUARTER, S)
+        dst = rounded(LAST).rearrange("p (c i t) -> p c t i", i=4, t=PACK)
+
+        def round_last(u, engine_copy):
+            engine_copy(dst[:, :, 2 * u : 2 * u + 2], last_acc[u][:].rearrange("p t (c i) -> p c t i", i=4))
+
+        def store_last(u, engine_copy):
+            engine_copy(res_last[:, 2 * u : 2 * u + 2, :], last_acc[u][:])
+            nc.sync.dma_start(out=out_rows[:, 2 * u : 2 * u + 2, js], in_=res_last[:, 2 * u : 2 * u + 2, :])
+
+        store_last(0, nc.scalar.copy)
+        round_last(0, nc.scalar.copy)
+        round_last(1, nc.vector.tensor_copy)
+        store_last(1, nc.vector.tensor_copy)
+        planes(HALF, HALF)
         for q in range(QUADS):
             queue = nc.sync if q % 2 else nc.scalar
             queue.dma_start(

@@ -22,6 +22,7 @@ QUADS = 4
 QUARTER = 128
 HALF = 256
 LAST = 3
+SCALAR_SHARE = 36
 
 
 def tile_picked_rvqres_none_po_kernel(
@@ -77,27 +78,30 @@ def tile_picked_rvqres_none_po_kernel(
         ws = new("ws", [P, N], U8)
         nc.gpsimd.memset(ws[:].bitcast(I32), 0)
         book_t = load_list("book_t", book)
-        offs_t = load_list("offs_t", offs)
         raw = {}
 
         def load_half(name, w, h):
-            raw[name, h] = new("%s_raw%d" % (name, h), [P, PACK, HALF], F32)
+            if name == "w1":
+                raw[name, h] = reused.tile([P, PACK, HALF], F32, name="w1_raw%d" % h, offset=4096 * h, align_bytes=64)
+            else:
+                raw[name, h] = new("%s_raw%d" % (name, h), [P, PACK, HALF], F32)
             nc.sync.dma_start(
                 out=raw[name, h][:],
                 in_=w.rearrange("(p j) c -> p j c", j=PACK)[:, :, h * HALF : (h + 1) * HALF],
             )
 
         load_half("w2", w2, 0)
+        offs_t = load_list("offs_t", offs)
         load_scale_rows(nc.sync, xs, 0, x_scales)
         load_half("w2", w2, 1)
         xw = new("xw", [P, T], I32)
         nc.sync.dma_start(out=xw[:], in_=words_of(x_words))
         c1_t = load_list("c1_t", c1)
+        c2_t = load_list("c2_t", c2)
         load_scale_rows(nc.sync, ws, 0, w3_scales)
         load_half("w1", w1, 0)
         load_half("w1", w1, 1)
         load_scale_rows(nc.sync, ws, 4, w4_scales)
-        c2_t = load_list("c2_t", c2)
         ww = new("ww", [P, 2, N], I32)
         nc.sync.dma_start(out=ww[:, 0, :], in_=words_of(w3_words))
         nc.sync.dma_start(out=ww[:, 1, :], in_=words_of(w4_words))
@@ -113,8 +117,10 @@ def tile_picked_rvqres_none_po_kernel(
             return dst, src
 
         w2_bf = new("w2_bf", [P, H * PACK], BF16)
-        for h in range(2):
-            nc.scalar.activation(*dealt_views(w2_bf, "w2", h), COPY)
+        nc.scalar.activation(*dealt_views(w2_bf, "w2", 0), COPY)
+        dst, src = dealt_views(w2_bf, "w2", 1)
+        nc.scalar.copy(dst[:, :SCALAR_SHARE], src[:, :SCALAR_SHARE])
+        nc.gpsimd.tensor_copy(dst[:, SCALAR_SHARE:], src[:, SCALAR_SHARE:])
         w2_codes = new("w2_codes", [P, H], U32)
         w2_sc = new("w2_sc", [P, H], U8)
         quantize(w2_codes[:], w2_sc[:], w2_bf[:])
@@ -135,28 +141,35 @@ def tile_picked_rvqres_none_po_kernel(
                 mm(acc[:], w2_codes[:, cols], w2_sc[:, cols], bw[:, lo:hi], bs[:, lo:hi])
                 parts.append((lo, hi, acc))
             c_parts.append(parts)
-        windows = [new("window%d" % t, [P, V], F32) for t in range(PACK)]
-        g1_halves = [new("g1_first", [P, PACK, HALF], F32)]
-        w1_bf = reused.tile([P, H * PACK], BF16, name="w1_bf", offset=2048, align_bytes=64)
+        windows, full = {}, {}
+        g1_half = new("g1_half", [P, PACK, HALF], F32)
+        w1_bf = reused.tile([P, H * PACK], BF16, name="w1_bf", offset=8192, align_bytes=64)
 
-        def first_lookup(h, t):
-            nc.vector.tensor_copy(g1_halves[h][:, t, :], windows[t][:].indirect(entries(c1_t, h * HALF, HALF)))
-
-        for t in range(PACK):
+        def first_lookup(t):
+            if t == LAST:
+                windows[t] = reused.tile([P, V], F32, name="window%d" % t, offset=4096, align_bytes=64)
+            else:
+                windows[t] = new("window%d" % t, [P, V], F32)
             for lo, hi, acc in c_parts[t]:
                 nc.scalar.activation(windows[t][:, lo:hi], acc[:], COPY, scale=-0.5)
-            first_lookup(0, t)
-        for h in range(2):
-            dst, src = dealt_views(w1_bf, "w1", h)
-            for a in range(0, 64, 32):
-                nc.gpsimd.tensor_copy(dst[:, a : a + 32], src[:, a : a + 32])
+            nc.vector.tensor_copy(g1_half[:, t, :], windows[t][:].indirect(entries(c1_t, 0, HALF)))
+
+        for t in range(LAST):
+            first_lookup(t)
+        for n in range(4):
+            dst, src = dealt_views(w1_bf, "w1", n // 2)
+            ms = slice(32 * (n % 2), 32 * (n % 2) + 32)
+            engine_copy = nc.scalar.copy if n == LAST else nc.gpsimd.tensor_copy
+            engine_copy(dst[:, ms], src[:, ms])
         w1_codes = new("w1_codes", [P, H], U32)
         w1_sc = new("w1_sc", [P, H], U8)
         quantize(w1_codes[:], w1_sc[:], w1_bf[:])
-        g1_halves.append(reused.tile([P, PACK, HALF], F32, name="g1_second", offset=0, align_bytes=64))
+        first_lookup(LAST)
         for t in range(PACK):
-            first_lookup(1, t)
-        g1 = [g1_halves[q // 2][:, :, q % 2 * QUARTER : (q % 2 + 1) * QUARTER] for q in range(4)]
+            full[t] = reused.tile([P, V], F32, name="full%d" % t, offset=(0, 2048, 8192, 6144)[t], align_bytes=64)
+            for lo, hi, acc in c_parts[t]:
+                nc.scalar.activation(full[t][:, lo:hi], acc[:], COPY, scale=-1.0)
+        g1 = [g1_half[:, :, q * QUARTER : (q + 1) * QUARTER] for q in range(2)]
         y = []
         for q in range(4):
             acc = bank(4 + q, "y_acc%d" % q, [P, PACK, QUARTER])
@@ -166,7 +179,7 @@ def tile_picked_rvqres_none_po_kernel(
                 mm(acc[:, t, :], w1_codes[:, cols], w1_sc[:, cols], pw[:, js], ps[:, js])
             y.append(acc)
 
-        wd_both = reused.tile([P, 2, N], I32, name="wd_both", offset=4096, align_bytes=64)
+        wd_both = reused.tile([P, 2, N], I32, name="wd_both", offset=10240, align_bytes=64)
         wd = [wd_both[:, w, :] for w in range(2)]
         for w in range(2):
             nc.gpsimd.tensor_copy(
@@ -199,9 +212,19 @@ def tile_picked_rvqres_none_po_kernel(
         r1 = {}
 
         def first_residual(q, tag=None):
-            r1[q] = new("r1_%d" % q, [P, PACK, QUARTER], F32, tag)
-            nc.vector.scalar_tensor_tensor(r1[q][:], g1[q], 2.0, y[q][:], MULT, ADD)
-            nc.scalar.copy(*woven(rz_bf[q][:, 0, :], r1[q][:]))
+            r1[q] = new("r1_%d" % q, [P, PACK, QUARTER], F32, tag)[:]
+            nc.vector.scalar_tensor_tensor(r1[q], g1[q], 2.0, y[q][:], MULT, ADD)
+            nc.scalar.copy(*woven(rz_bf[q][:, 0, :], r1[q]))
+
+        def fused_residuals(tag):
+            tile = new("r1_half", [P, PACK, HALF], F32, tag)
+            for t in range(PACK):
+                nc.vector.tensor_tensor(
+                    tile[:, t, :], full[t][:].indirect(entries(c1_t, HALF, HALF)), y_half[:, t, :], ADD
+                )
+            for q in range(2, 4):
+                r1[q] = tile[:, :, (q - 2) * QUARTER : (q - 1) * QUARTER]
+                nc.scalar.copy(*woven(rz_bf[q][:, 0, :], r1[q]))
 
         def second_residual(q, tag=None):
             z = new("z_%d" % q, [P, PACK, QUARTER], F32, tag)
@@ -251,23 +274,32 @@ def tile_picked_rvqres_none_po_kernel(
             quantize_residuals(q, both)
             open_product(q)
             close_product(q)
-            nc.vector.tensor_copy(*woven(rounded(q), res[q][:]))
+            if q < 2:
+                nc.scalar.copy(*woven(rounded(q), out_acc[q][:]))
+            else:
+                nc.vector.tensor_copy(*woven(rounded(q), res[q][:]))
 
         first_residual(0)
         first_residual(1)
+        y_half = new("y_half", [P, PACK, HALF], F32)
+        for q in range(2, 4):
+            nc.scalar.copy(y_half[:, :, (q - 2) * QUARTER : (q - 1) * QUARTER], y[q][:])
         second_residual(0)
-        first_residual(2)
-        finish(0)
         second_residual(1)
-        first_residual(3)
+        finish(0)
         finish(1)
+        warm = bank(1, "warm", [P, S])
+        for t in range(2):
+            cols = slice(t * P, (t + 1) * P)
+            mm(warm[:], w1_codes[:, cols], w1_sc[:, cols], pw[:], ps[:])
+        fused_residuals("rz_bf0")
         second_residual(2)
+        second_residual(LAST)
         finish(2)
         quantize_residuals(LAST, only_r1)
         last_acc = [bank(3 + u, "last_acc%d" % u, [P, 2, QUARTER]) for u in range(2)]
         for u in range(2):
             passes(last_acc[u], LAST, 0, (2 * u, 2 * u + 1), True, False)
-        second_residual(LAST)
         quantize_residuals(LAST, only_z)
         for u in range(2):
             passes(last_acc[u], LAST, 1, (2 * u, 2 * u + 1), False, True)

@@ -23,6 +23,7 @@ QUARTER = 128
 HALF = 256
 LAST = 3
 SCALAR_SHARE = 36
+W1_SCALAR_SHARE = 36
 
 
 def tile_picked_rvqres_none_po_kernel(
@@ -98,9 +99,9 @@ def tile_picked_rvqres_none_po_kernel(
         nc.sync.dma_start(out=xw[:], in_=words_of(x_words))
         c1_t = load_list("c1_t", c1)
         c2_t = load_list("c2_t", c2)
-        load_scale_rows(nc.sync, ws, 0, w3_scales)
         load_half("w1", w1, 0)
         load_half("w1", w1, 1)
+        load_scale_rows(nc.sync, ws, 0, w3_scales)
         load_scale_rows(nc.sync, ws, 4, w4_scales)
         ww = new("ww", [P, 2, N], I32)
         nc.sync.dma_start(out=ww[:, 0, :], in_=words_of(w3_words))
@@ -134,7 +135,7 @@ def tile_picked_rvqres_none_po_kernel(
         c_parts = []
         for t in range(PACK):
             cols = slice(t * P, (t + 1) * P)
-            spans = ((0, HALF, 4), (HALF, V, 0)) if t == 0 else ((0, V, t),)
+            spans = ((0, HALF, 7), (HALF, V, 0)) if t == 0 else ((0, V, t),)
             parts = []
             for lo, hi, b in spans:
                 acc = bank(b, "c_acc%d_%d" % (t, lo), [P, hi - lo])
@@ -143,7 +144,7 @@ def tile_picked_rvqres_none_po_kernel(
             c_parts.append(parts)
         windows, full = {}, {}
         g1_half = new("g1_half", [P, PACK, HALF], F32)
-        w1_bf = reused.tile([P, H * PACK], BF16, name="w1_bf", offset=8192, align_bytes=64)
+        w1_bf = reused.tile([P, H * PACK], BF16, name="w1_bf", offset=10240, align_bytes=64)
 
         def first_lookup(t):
             if t == LAST:
@@ -156,30 +157,31 @@ def tile_picked_rvqres_none_po_kernel(
 
         for t in range(LAST):
             first_lookup(t)
-        for n in range(4):
-            dst, src = dealt_views(w1_bf, "w1", n // 2)
-            ms = slice(32 * (n % 2), 32 * (n % 2) + 32)
-            engine_copy = nc.scalar.copy if n == LAST else nc.gpsimd.tensor_copy
-            engine_copy(dst[:, ms], src[:, ms])
+        nc.gpsimd.tensor_copy(*dealt_views(w1_bf, "w1", 0))
+        dst, src = dealt_views(w1_bf, "w1", 1)
+        nc.scalar.copy(dst[:, :W1_SCALAR_SHARE], src[:, :W1_SCALAR_SHARE])
+        nc.gpsimd.tensor_copy(dst[:, W1_SCALAR_SHARE:], src[:, W1_SCALAR_SHARE:])
         w1_codes = new("w1_codes", [P, H], U32)
         w1_sc = new("w1_sc", [P, H], U8)
-        quantize(w1_codes[:], w1_sc[:], w1_bf[:])
+        for a in range(0, H, HALF):
+            quantize(w1_codes[:, a : a + HALF], w1_sc[:, a : a + HALF], w1_bf[:, a * PACK : (a + HALF) * PACK])
         first_lookup(LAST)
         for t in range(PACK):
-            full[t] = reused.tile([P, V], F32, name="full%d" % t, offset=(0, 2048, 8192, 6144)[t], align_bytes=64)
-            for lo, hi, acc in c_parts[t]:
-                nc.scalar.activation(full[t][:, lo:hi], acc[:], COPY, scale=-1.0)
-        g1 = [g1_half[:, :, q * QUARTER : (q + 1) * QUARTER] for q in range(2)]
-        y = []
-        for q in range(4):
-            acc = bank(4 + q, "y_acc%d" % q, [P, PACK, QUARTER])
-            js = slice(q * QUARTER, (q + 1) * QUARTER)
-            for t in range(PACK):
-                cols = slice(t * P, (t + 1) * P)
-                mm(acc[:, t, :], w1_codes[:, cols], w1_sc[:, cols], pw[:, js], ps[:, js])
-            y.append(acc)
+            full[t] = reused.tile([P, V], F32, name="full%d" % t, offset=(1024, 10240, 12288, 6144)[t], align_bytes=64)
+            if t == 0:
+                nc.gpsimd.tensor_scalar(full[t][:], windows[t][:], 2.0, 0.0, MULT, ADD)
+            else:
+                nc.scalar.activation(full[t][:], c_parts[t][0][2][:], COPY, scale=-1.0)
+        y = {}
+        for h in range(2):
+            js = slice(h * HALF, (h + 1) * HALF)
+            for u in range(2):
+                y[h, u] = bank(4 + 2 * h + u, "y_acc%d_%d" % (h, u), [P, 2, HALF])
+                for n in range(2):
+                    cols = slice((2 * u + n) * P, (2 * u + n + 1) * P)
+                    mm(y[h, u][:, n, :], w1_codes[:, cols], w1_sc[:, cols], pw[:, js], ps[:, js])
 
-        wd_both = reused.tile([P, 2, N], I32, name="wd_both", offset=10240, align_bytes=64)
+        wd_both = new("wd_both", [P, 2, N], I32)
         wd = [wd_both[:, w, :] for w in range(2)]
         for w in range(2):
             nc.gpsimd.tensor_copy(
@@ -211,10 +213,14 @@ def tile_picked_rvqres_none_po_kernel(
 
         r1 = {}
 
-        def first_residual(q, tag=None):
-            r1[q] = new("r1_%d" % q, [P, PACK, QUARTER], F32, tag)[:]
-            nc.vector.scalar_tensor_tensor(r1[q], g1[q], 2.0, y[q][:], MULT, ADD)
-            nc.scalar.copy(*woven(rz_bf[q][:, 0, :], r1[q]))
+        def summed_residuals():
+            tile = new("r1_first", [P, PACK, HALF], F32)
+            for u in range(2):
+                ts = slice(2 * u, 2 * u + 2)
+                nc.vector.scalar_tensor_tensor(tile[:, ts, :], g1_half[:, ts, :], 2.0, y[0, u][:], MULT, ADD)
+            for q in range(2):
+                r1[q] = tile[:, :, q * QUARTER : (q + 1) * QUARTER]
+                nc.scalar.copy(*woven(rz_bf[q][:, 0, :], r1[q]))
 
         def fused_residuals(tag):
             tile = new("r1_half", [P, PACK, HALF], F32, tag)
@@ -276,23 +282,20 @@ def tile_picked_rvqres_none_po_kernel(
             close_product(q)
             if q < 2:
                 nc.scalar.copy(*woven(rounded(q), out_acc[q][:]))
-            else:
-                nc.vector.tensor_copy(*woven(rounded(q), res[q][:]))
 
-        first_residual(0)
-        first_residual(1)
+        summed_residuals()
         y_half = new("y_half", [P, PACK, HALF], F32)
-        for q in range(2, 4):
-            nc.scalar.copy(y_half[:, :, (q - 2) * QUARTER : (q - 1) * QUARTER], y[q][:])
+        for u in range(2):
+            nc.scalar.copy(y_half[:, 2 * u : 2 * u + 2, :], y[1, u][:])
         second_residual(0)
         second_residual(1)
         finish(0)
         finish(1)
         warm = bank(1, "warm", [P, S])
-        for t in range(2):
+        for t in range(3):
             cols = slice(t * P, (t + 1) * P)
             mm(warm[:], w1_codes[:, cols], w1_sc[:, cols], pw[:], ps[:])
-        fused_residuals("rz_bf0")
+        fused_residuals("z_0")
         second_residual(2)
         second_residual(LAST)
         finish(2)
@@ -315,10 +318,11 @@ def tile_picked_rvqres_none_po_kernel(
             engine_copy(res_last[:, 2 * u : 2 * u + 2, :], last_acc[u][:])
             nc.sync.dma_start(out=out_rows[:, 2 * u : 2 * u + 2, js], in_=res_last[:, 2 * u : 2 * u + 2, :])
 
-        store_last(0, nc.scalar.copy)
         round_last(0, nc.scalar.copy)
         round_last(1, nc.vector.tensor_copy)
-        store_last(1, nc.vector.tensor_copy)
+        nc.vector.tensor_copy(*woven(rounded(2), res[2][:]))
+        store_last(0, nc.scalar.copy)
+        store_last(1, nc.scalar.copy)
         planes(HALF, HALF)
         for q in range(QUADS):
             queue = nc.sync if q % 2 else nc.scalar

@@ -49,8 +49,8 @@ def tile_picked_rvqres_none_po_kernel(
         def load_scale_rows(queue, tile, first_row, src):
             for q in range(QUADS):
                 queue.dma_start(
-                    out=tile[32 * q + first_row : 32 * q + first_row + 4, :].bitcast(I32),
-                    in_=src[0, 4 * q : 4 * q + 4, :].bitcast(I32),
+                    out=tile[first_row + q : P : 32, :].bitcast(I32),
+                    in_=src[0, q : 16 : 4, :].bitcast(I32),
                 )
 
         def words_of(src):

@@ -23,7 +23,7 @@ QUARTER = 128
 HALF = 256
 LAST = 3
 SCALAR_SHARE = 36
-W1_SCALAR_SHARE = 36
+PAIR = 2
 
 
 def tile_picked_rvqres_none_po_kernel(
@@ -38,6 +38,9 @@ def tile_picked_rvqres_none_po_kernel(
         def new(name, shape, dtype, tag=None):
             return keep.tile(shape, dtype, name=name, tag=tag or name, align_bytes=64)
 
+        def placed(name, shape, dtype, offset):
+            return reused.tile(shape, dtype, name=name, offset=offset, align_bytes=64)
+
         def bank(index, name, shape):
             return psum.tile(shape, F32, name=name, tag="bank%d" % index)
 
@@ -46,11 +49,11 @@ def tile_picked_rvqres_none_po_kernel(
             nc.sync.dma_start(tile[:], src)
             return tile
 
-        def load_scale_rows(queue, tile, first_row, src):
-            for q in range(QUADS):
-                queue.dma_start(
-                    out=tile[first_row + q : P : 32, :].bitcast(I32),
-                    in_=src[0, q : 16 : 4, :].bitcast(I32),
+        def load_scale_rows(tile, first_row, src):
+            for r in range(PACK):
+                nc.sync.dma_start(
+                    out=tile[first_row + r : P : 32, :].bitcast(I32),
+                    in_=src[0, r : 16 : 4, :].bitcast(I32),
                 )
 
         def words_of(src):
@@ -68,11 +71,11 @@ def tile_picked_rvqres_none_po_kernel(
                 rhs=rhs_codes.bitcast(FP8X4), rhs_scale=rhs_scales, start=start, stop=stop,
             )
 
-        def woven(grouped, planes):
-            return (
-                grouped.rearrange("p (c i t) -> p c t i", i=4, t=PACK),
-                planes.rearrange("p t (c i) -> p c t i", i=4),
-            )
+        def as_words(grouped):
+            return grouped.rearrange("p (c i t) -> p c t i", i=PAIR, t=PACK)
+
+        def as_planes(planes):
+            return planes.rearrange("p t (c i) -> p c t i", i=PAIR)
 
         xs = new("xs", [P, T], U8)
         nc.vector.memset(xs[:].bitcast(I32), 0)
@@ -82,10 +85,7 @@ def tile_picked_rvqres_none_po_kernel(
         raw = {}
 
         def load_half(name, w, h):
-            if name == "w1":
-                raw[name, h] = reused.tile([P, PACK, HALF], F32, name="w1_raw%d" % h, offset=4096 * h, align_bytes=64)
-            else:
-                raw[name, h] = new("%s_raw%d" % (name, h), [P, PACK, HALF], F32)
+            raw[name, h] = new("%s_raw%d" % (name, h), [P, PACK, HALF], F32)
             nc.sync.dma_start(
                 out=raw[name, h][:],
                 in_=w.rearrange("(p j) c -> p j c", j=PACK)[:, :, h * HALF : (h + 1) * HALF],
@@ -93,7 +93,7 @@ def tile_picked_rvqres_none_po_kernel(
 
         load_half("w2", w2, 0)
         offs_t = load_list("offs_t", offs)
-        load_scale_rows(nc.sync, xs, 0, x_scales)
+        load_scale_rows(xs, 0, x_scales)
         load_half("w2", w2, 1)
         xw = new("xw", [P, T], I32)
         nc.sync.dma_start(out=xw[:], in_=words_of(x_words))
@@ -101,8 +101,8 @@ def tile_picked_rvqres_none_po_kernel(
         c2_t = load_list("c2_t", c2)
         load_half("w1", w1, 0)
         load_half("w1", w1, 1)
-        load_scale_rows(nc.sync, ws, 0, w3_scales)
-        load_scale_rows(nc.sync, ws, 4, w4_scales)
+        load_scale_rows(ws, 0, w3_scales)
+        load_scale_rows(ws, 4, w4_scales)
         ww = new("ww", [P, 2, N], I32)
         nc.sync.dma_start(out=ww[:, 0, :], in_=words_of(w3_words))
         nc.sync.dma_start(out=ww[:, 1, :], in_=words_of(w4_words))
@@ -142,57 +142,66 @@ def tile_picked_rvqres_none_po_kernel(
                 mm(acc[:], w2_codes[:, cols], w2_sc[:, cols], bw[:, lo:hi], bs[:, lo:hi])
                 parts.append((lo, hi, acc))
             c_parts.append(parts)
-        windows, full = {}, {}
-        g1_half = new("g1_half", [P, PACK, HALF], F32)
-        w1_bf = reused.tile([P, H * PACK], BF16, name="w1_bf", offset=10240, align_bytes=64)
 
-        def first_lookup(t):
-            if t == LAST:
-                windows[t] = reused.tile([P, V], F32, name="window%d" % t, offset=4096, align_bytes=64)
-            else:
-                windows[t] = new("window%d" % t, [P, V], F32)
+        windows = [new("window%d" % t, [P, V], F32) for t in range(PACK)]
+        g1 = [new("g1_%d" % h, [P, PACK, HALF], F32) for h in range(2)]
+        g2 = new("g2", [P, PACK, HALF], F32)
+
+        def scalar_window(t):
             for lo, hi, acc in c_parts[t]:
                 nc.scalar.activation(windows[t][:, lo:hi], acc[:], COPY, scale=-0.5)
-            nc.vector.tensor_copy(g1_half[:, t, :], windows[t][:].indirect(entries(c1_t, 0, HALF)))
 
-        for t in range(LAST):
-            first_lookup(t)
-        nc.gpsimd.tensor_copy(*dealt_views(w1_bf, "w1", 0))
-        dst, src = dealt_views(w1_bf, "w1", 1)
-        nc.scalar.copy(dst[:, :W1_SCALAR_SHARE], src[:, :W1_SCALAR_SHARE])
-        nc.gpsimd.tensor_copy(dst[:, W1_SCALAR_SHARE:], src[:, W1_SCALAR_SHARE:])
-        w1_codes = new("w1_codes", [P, H], U32)
-        w1_sc = new("w1_sc", [P, H], U8)
-        for a in range(0, H, HALF):
-            quantize(w1_codes[:, a : a + HALF], w1_sc[:, a : a + HALF], w1_bf[:, a * PACK : (a + HALF) * PACK])
-        first_lookup(LAST)
-        for t in range(PACK):
-            full[t] = reused.tile([P, V], F32, name="full%d" % t, offset=(1024, 10240, 12288, 6144)[t], align_bytes=64)
-            if t == 0:
-                nc.gpsimd.tensor_scalar(full[t][:], windows[t][:], 2.0, 0.0, MULT, ADD)
-            else:
-                nc.scalar.activation(full[t][:], c_parts[t][0][2][:], COPY, scale=-1.0)
-        y = {}
+        def first_lookup(t, h):
+            nc.scalar.activation(g1[h][:, t, :], windows[t][:].indirect(entries(c1_t, h * HALF, HALF)), COPY, scale=2.0)
+
+        def second_lookup_view(t, h):
+            return windows[t][:].indirect(entries(c2_t, h * HALF, HALF))
+
+        scalar_window(0)
+        nc.vector.tensor_scalar(windows[1][:], c_parts[1][0][2][:], -0.5, None, MULT)
+        first_lookup(0, 0)
+        scalar_window(2)
+        for t in range(2):
+            nc.vector.tensor_copy(g2[:, t, :], second_lookup_view(t, 1))
+        first_lookup(1, 0)
+        scalar_window(3)
+        first_lookup(2, 0)
+        first_lookup(3, 0)
+
+        w1_bf = placed("w1_bf", [P, H * PACK], BF16, 0)
         for h in range(2):
-            js = slice(h * HALF, (h + 1) * HALF)
-            for u in range(2):
-                y[h, u] = bank(4 + 2 * h + u, "y_acc%d_%d" % (h, u), [P, 2, HALF])
-                for n in range(2):
-                    cols = slice((2 * u + n) * P, (2 * u + n + 1) * P)
-                    mm(y[h, u][:, n, :], w1_codes[:, cols], w1_sc[:, cols], pw[:, js], ps[:, js])
+            nc.gpsimd.tensor_copy(*dealt_views(w1_bf, "w1", h))
+        w1_codes = placed("w1_codes", [P, H], U32, 4096)
+        w1_sc = new("w1_sc", [P, H], U8)
+        quantize(w1_codes[:], w1_sc[:], w1_bf[:])
+        y = []
+        for q in range(QUADS):
+            js = slice(q * QUARTER, (q + 1) * QUARTER)
+            y.append(bank(4 + q, "y_acc%d" % q, [P, PACK, QUARTER]))
+            for t in range(PACK):
+                cols = slice(t * P, (t + 1) * P)
+                mm(y[q][:, t, :], w1_codes[:, cols], w1_sc[:, cols], pw[:, js], ps[:, js])
 
-        wd_both = new("wd_both", [P, 2, N], I32)
+        both_lookups = placed("both_lookups", [P, PACK, HALF], F32, 0)
+        for t in range(PACK):
+            nc.vector.tensor_tensor(both_lookups[:, t, :], second_lookup_view(t, 0), g1[0][:, t, :], ADD)
+        for t in range(PACK):
+            first_lookup(t, 1)
+        for t in range(2, PACK):
+            nc.scalar.activation(g2[:, t, :], second_lookup_view(t, 1), COPY)
+
+        wsd = placed("wsd", [P, N], U8, 4096)
+        nc.gpsimd.tensor_copy(
+            wsd[:].rearrange("p (t m) -> p t m", t=PACK),
+            ws[:].rearrange("p (m t) -> p t m", t=PACK),
+        )
+        wd_both = placed("wd_both", [P, 2, N], I32, 4096 + N)
         wd = [wd_both[:, w, :] for w in range(2)]
         for w in range(2):
             nc.gpsimd.tensor_copy(
                 wd[w].rearrange("p (t c i) -> p c t i", t=PACK, i=4),
                 ww[:, w, :].rearrange("p (c i t) -> p c t i", t=PACK, i=4),
             )
-        wsd = new("wsd", [P, N], U8)
-        nc.gpsimd.tensor_copy(
-            wsd[:].rearrange("p (t m) -> p t m", t=PACK),
-            ws[:].rearrange("p (m t) -> p t m", t=PACK),
-        )
 
         out_codes = new("out_codes", [P, S], I32)
         out_scales = new("out_scales", [P, S], U8)
@@ -200,9 +209,9 @@ def tile_picked_rvqres_none_po_kernel(
         out_words = words_of(out_1)
         out_bf = new("out_bf", [P, S * PACK], BF16)
 
-        rz_bf = [new("rz_bf%d" % q, [P, 2, QUARTER * PACK], BF16) for q in range(4)]
-        rz_codes = [new("rz_codes%d" % q, [P, 2, QUARTER], U32) for q in range(4)]
-        rz_scales = [new("rz_scales%d" % q, [P, 2, QUARTER], U8) for q in range(4)]
+        rz_bf = [new("rz_bf%d" % q, [P, 2, QUARTER * PACK], BF16) for q in range(QUADS)]
+        rz_codes = [new("rz_codes%d" % q, [P, 2, QUARTER], U32) for q in range(QUADS)]
+        rz_scales = [new("rz_scales%d" % q, [P, 2, QUARTER], U8) for q in range(QUADS)]
 
         def quantize_residuals(q, which):
             quantize(
@@ -211,37 +220,18 @@ def tile_picked_rvqres_none_po_kernel(
                 rz_bf[q][:, which, :].rearrange("p a n -> p (a n)"),
             )
 
+        def quarter_of(tile, q):
+            return tile[:, :, (q % 2) * QUARTER : (q % 2 + 1) * QUARTER]
+
+        def woven_sum(q, which, left, right):
+            nc.vector.tensor_tensor(as_words(rz_bf[q][:, which, :]), as_planes(left), as_planes(right), ADD)
+
         r1 = {}
 
-        def summed_residuals():
-            tile = new("r1_first", [P, PACK, HALF], F32)
-            for u in range(2):
-                ts = slice(2 * u, 2 * u + 2)
-                nc.vector.scalar_tensor_tensor(tile[:, ts, :], g1_half[:, ts, :], 2.0, y[0, u][:], MULT, ADD)
-            for q in range(2):
-                r1[q] = tile[:, :, q * QUARTER : (q + 1) * QUARTER]
-                nc.scalar.copy(*woven(rz_bf[q][:, 0, :], r1[q]))
-
-        def fused_residuals(tag):
-            tile = new("r1_half", [P, PACK, HALF], F32, tag)
-            for t in range(PACK):
-                nc.vector.tensor_tensor(
-                    tile[:, t, :], full[t][:].indirect(entries(c1_t, HALF, HALF)), y_half[:, t, :], ADD
-                )
-            for q in range(2, 4):
-                r1[q] = tile[:, :, (q - 2) * QUARTER : (q - 1) * QUARTER]
-                nc.scalar.copy(*woven(rz_bf[q][:, 0, :], r1[q]))
-
-        def second_residual(q, tag=None):
-            z = new("z_%d" % q, [P, PACK, QUARTER], F32, tag)
-            for t in range(PACK):
-                nc.vector.tensor_tensor(
-                    z[:, t, :], windows[t][:].indirect(entries(c2_t, q * QUARTER, QUARTER)), r1[q][:, t, :], ADD
-                )
-            dst, src = woven(rz_bf[q][:, 1, :], z[:])
-            step = 2 if q == LAST else PACK
-            for t in range(0, PACK, step):
-                nc.scalar.copy(dst[:, :, t : t + step], src[:, :, t : t + step])
+        def first_residual(q):
+            r1[q] = new("r1_%d" % q, [P, PACK, QUARTER], F32)
+            nc.vector.tensor_tensor(r1[q][:], y[q][:], quarter_of(g1[1], q), ADD)
+            nc.scalar.copy(as_words(rz_bf[q][:, 0, :]), as_planes(r1[q][:]))
 
         def passes(acc, q, which, planes, start, stop):
             for n, t in enumerate(planes):
@@ -255,50 +245,36 @@ def tile_picked_rvqres_none_po_kernel(
         def rounded(q):
             return out_bf[:, q * QUARTER * PACK : (q + 1) * QUARTER * PACK]
 
-        out_acc = {}
-
-        def open_product(q):
-            out_acc[q] = bank(q, "out_acc%d" % q, [P, PACK, QUARTER])
-            passes(out_acc[q], q, 0, range(PACK), True, False)
-
         res = {}
+        both, only_r1, only_z = slice(0, 2), slice(0, 1), slice(1, 2)
 
-        def close_product(q):
-            passes(out_acc[q], q, 1, range(PACK), False, True)
+        def product(q):
+            quantize_residuals(q, both)
+            acc = bank(q, "out_acc%d" % q, [P, PACK, QUARTER])
+            passes(acc, q, 0, range(PACK), True, False)
+            passes(acc, q, 1, range(PACK), False, True)
             res[q] = new("res%d" % q, [P, PACK, QUARTER], F32)
-            nc.scalar.copy(res[q][:], out_acc[q][:])
+            nc.scalar.copy(res[q][:], acc[:])
             nc.sync.dma_start(out=out_rows[:, :, q * QUARTER : (q + 1) * QUARTER], in_=res[q][:])
+            if q < 2:
+                nc.scalar.copy(as_words(rounded(q)), as_planes(acc[:]))
 
         def planes(start, count):
             js = slice(start, start + count)
             quantize(out_codes[:, js], out_scales[:, js], out_bf[:, start * PACK : (start + count) * PACK])
             nc.sync.dma_start(out=out_words[:, js], in_=out_codes[:, js])
 
-        both, only_r1, only_z = slice(0, 2), slice(0, 1), slice(1, 2)
-
-        def finish(q):
-            quantize_residuals(q, both)
-            open_product(q)
-            close_product(q)
-            if q < 2:
-                nc.scalar.copy(*woven(rounded(q), out_acc[q][:]))
-
-        summed_residuals()
-        y_half = new("y_half", [P, PACK, HALF], F32)
-        for u in range(2):
-            nc.scalar.copy(y_half[:, 2 * u : 2 * u + 2, :], y[1, u][:])
-        second_residual(0)
-        second_residual(1)
-        finish(0)
-        finish(1)
-        warm = bank(1, "warm", [P, S])
-        for t in range(3):
-            cols = slice(t * P, (t + 1) * P)
-            mm(warm[:], w1_codes[:, cols], w1_sc[:, cols], pw[:], ps[:])
-        fused_residuals("z_0")
-        second_residual(2)
-        second_residual(LAST)
-        finish(2)
+        woven_sum(0, 0, y[0][:], quarter_of(g1[0], 0))
+        woven_sum(0, 1, y[0][:], quarter_of(both_lookups, 0))
+        woven_sum(1, 0, y[1][:], quarter_of(g1[0], 1))
+        product(0)
+        woven_sum(1, 1, y[1][:], quarter_of(both_lookups, 1))
+        first_residual(2)
+        product(1)
+        woven_sum(2, 1, r1[2][:], quarter_of(g2, 2))
+        first_residual(LAST)
+        product(2)
+        woven_sum(LAST, 1, r1[LAST][:], quarter_of(g2, LAST))
         quantize_residuals(LAST, only_r1)
         last_acc = [bank(3 + u, "last_acc%d" % u, [P, 2, QUARTER]) for u in range(2)]
         for u in range(2):
@@ -309,18 +285,18 @@ def tile_picked_rvqres_none_po_kernel(
         planes(0, HALF)
         res_last = new("res_last", [P, PACK, QUARTER], F32)
         js = slice(LAST * QUARTER, S)
-        dst = rounded(LAST).rearrange("p (c i t) -> p c t i", i=4, t=PACK)
+        dst = as_words(rounded(LAST))
 
         def round_last(u, engine_copy):
-            engine_copy(dst[:, :, 2 * u : 2 * u + 2], last_acc[u][:].rearrange("p t (c i) -> p c t i", i=4))
+            engine_copy(dst[:, :, 2 * u : 2 * u + 2], as_planes(last_acc[u][:]))
 
         def store_last(u, engine_copy):
             engine_copy(res_last[:, 2 * u : 2 * u + 2, :], last_acc[u][:])
             nc.sync.dma_start(out=out_rows[:, 2 * u : 2 * u + 2, js], in_=res_last[:, 2 * u : 2 * u + 2, :])
 
+        nc.vector.tensor_copy(as_words(rounded(2)), as_planes(res[2][:]))
         round_last(0, nc.scalar.copy)
         round_last(1, nc.vector.tensor_copy)
-        nc.vector.tensor_copy(*woven(rounded(2), res[2][:]))
         store_last(0, nc.scalar.copy)
         store_last(1, nc.scalar.copy)
         planes(HALF, HALF)

@@ -197,11 +197,10 @@ def tile_picked_rvqres_none_po_kernel(
         )
         wd_both = placed("wd_both", [P, 2, N], I32, 4096 + N)
         wd = [wd_both[:, w, :] for w in range(2)]
-        for w in range(2):
-            nc.gpsimd.tensor_copy(
-                wd[w].rearrange("p (t c i) -> p c t i", t=PACK, i=4),
-                ww[:, w, :].rearrange("p (c i t) -> p c t i", t=PACK, i=4),
-            )
+        nc.gpsimd.tensor_copy(
+            wd_both[:].rearrange("p w (t c i) -> p w c t i", t=PACK, i=4),
+            ww[:].rearrange("p w (c i t) -> p w c t i", t=PACK, i=4),
+        )
 
         out_codes = new("out_codes", [P, S], I32)
         out_scales = new("out_scales", [P, S], U8)
@@ -209,8 +208,10 @@ def tile_picked_rvqres_none_po_kernel(
         out_words = words_of(out_1)
         out_bf = new("out_bf", [P, S * PACK], BF16)
 
-        rz_bf = [new("rz_bf%d" % q, [P, 2, QUARTER * PACK], BF16) for q in range(QUADS)]
-        rz_codes = [new("rz_codes%d" % q, [P, 2, QUARTER], U32) for q in range(QUADS)]
+        rz_bf = [new("rz_bf%d" % q, [P, 2, QUARTER * PACK], BF16) for q in range(2)]
+        rz_codes = [placed("rz_codes%d" % q, [P, 2, QUARTER], U32, 12288 + 8192 * q) for q in range(2)]
+        rz_bf.extend(placed("rz_bf%d" % q, [P, 2, QUARTER * PACK], BF16, 12288 + 2048 * (q - 2) - 1536) for q in range(2, QUADS))
+        rz_codes.extend(new("rz_codes%d" % q, [P, 2, QUARTER], U32) for q in range(2, QUADS))
         rz_scales = [new("rz_scales%d" % q, [P, 2, QUARTER], U8) for q in range(QUADS)]
 
         def quantize_residuals(q, which):
@@ -231,7 +232,9 @@ def tile_picked_rvqres_none_po_kernel(
         def first_residual(q):
             r1[q] = new("r1_%d" % q, [P, PACK, QUARTER], F32)
             nc.vector.tensor_tensor(r1[q][:], y[q][:], quarter_of(g1[1], q), ADD)
-            nc.scalar.copy(as_words(rz_bf[q][:, 0, :]), as_planes(r1[q][:]))
+
+        def weave_first_residual(q, engine_copy):
+            engine_copy(as_words(rz_bf[q][:, 0, :]), as_planes(r1[q][:]))
 
         def passes(acc, q, which, planes, start, stop):
             for n, t in enumerate(planes):
@@ -256,8 +259,6 @@ def tile_picked_rvqres_none_po_kernel(
             res[q] = new("res%d" % q, [P, PACK, QUARTER], F32)
             nc.scalar.copy(res[q][:], acc[:])
             nc.sync.dma_start(out=out_rows[:, :, q * QUARTER : (q + 1) * QUARTER], in_=res[q][:])
-            if q < 2:
-                nc.scalar.copy(as_words(rounded(q)), as_planes(acc[:]))
 
         def planes(start, count):
             js = slice(start, start + count)
@@ -270,19 +271,22 @@ def tile_picked_rvqres_none_po_kernel(
         product(0)
         woven_sum(1, 1, y[1][:], quarter_of(both_lookups, 1))
         first_residual(2)
+        weave_first_residual(2, nc.scalar.copy)
         product(1)
-        woven_sum(2, 1, r1[2][:], quarter_of(g2, 2))
         first_residual(LAST)
+        woven_sum(2, 1, r1[2][:], quarter_of(g2, 2))
+        weave_first_residual(LAST, nc.vector.tensor_copy)
+        nc.scalar.copy(as_words(rounded(0)), as_planes(res[0][:]))
         product(2)
-        woven_sum(LAST, 1, r1[LAST][:], quarter_of(g2, LAST))
         quantize_residuals(LAST, only_r1)
+        woven_sum(LAST, 1, r1[LAST][:], quarter_of(g2, LAST))
         last_acc = [bank(3 + u, "last_acc%d" % u, [P, 2, QUARTER]) for u in range(2)]
         for u in range(2):
             passes(last_acc[u], LAST, 0, (2 * u, 2 * u + 1), True, False)
         quantize_residuals(LAST, only_z)
         for u in range(2):
             passes(last_acc[u], LAST, 1, (2 * u, 2 * u + 1), False, True)
-        planes(0, HALF)
+        nc.vector.tensor_copy(as_words(rounded(1)), as_planes(res[1][:]))
         res_last = new("res_last", [P, PACK, QUARTER], F32)
         js = slice(LAST * QUARTER, S)
         dst = as_words(rounded(LAST))
@@ -294,9 +298,10 @@ def tile_picked_rvqres_none_po_kernel(
             engine_copy(res_last[:, 2 * u : 2 * u + 2, :], last_acc[u][:])
             nc.sync.dma_start(out=out_rows[:, 2 * u : 2 * u + 2, js], in_=res_last[:, 2 * u : 2 * u + 2, :])
 
-        nc.vector.tensor_copy(as_words(rounded(2)), as_planes(res[2][:]))
         round_last(0, nc.scalar.copy)
         round_last(1, nc.vector.tensor_copy)
+        planes(0, HALF)
+        nc.vector.tensor_copy(as_words(rounded(2)), as_planes(res[2][:]))
         store_last(0, nc.scalar.copy)
         store_last(1, nc.scalar.copy)
         planes(HALF, HALF)

@@ -271,9 +271,9 @@ def tile_picked_rvqres_none_po_kernel(
         product(0)
         woven_sum(1, 1, y[1][:], quarter_of(both_lookups, 1))
         first_residual(2)
-        weave_first_residual(2, nc.scalar.copy)
         product(1)
         first_residual(LAST)
+        weave_first_residual(2, nc.vector.tensor_copy)
         woven_sum(2, 1, r1[2][:], quarter_of(g2, 2))
         weave_first_residual(LAST, nc.vector.tensor_copy)
         nc.scalar.copy(as_words(rounded(0)), as_planes(res[0][:]))

@@ -23,7 +23,7 @@ QUARTER = 128
 HALF = 256
 LAST = 3
 SCALAR_SHARE = 36
-PAIR = 2
+PAIR = 4
 
 
 def tile_picked_rvqres_none_po_kernel(

from contextlib import ExitStack

import concourse.mybir as mybir

K, T, S, V, H, N = 512, 2048, 512, 512, 512, 512
FLOPS = 2 * (K * H * S + K * H * V + 2 * H * N * S)

F32 = mybir.dt.float32
BF16 = mybir.dt.bfloat16
I32 = mybir.dt.int32
U32 = mybir.dt.uint32
U16 = mybir.dt.uint16
U8 = mybir.dt.uint8
FP8X4 = mybir.dt.float8_e4m3fn_x4
MULT = mybir.AluOpType.mult
ADD = mybir.AluOpType.add
COPY = mybir.ActivationFunctionType.Copy

P = 128
PACK = 4
QUADS = 4
QUARTER = 128
HALF = 256
LAST = 3
SCALAR_SHARE = 36
PAIR = 4


def tile_picked_rvqres_none_po_kernel(
    tc, x_words, x_scales, w1, w2, w3_words, w3_scales, w4_words, w4_scales, offs, book, c1, c2, out_0, out_1, out_2
):
    nc = tc.nc
    with ExitStack() as ctx:
        keep = ctx.enter_context(tc.tile_pool(name="keep", bufs=1))
        reused = ctx.enter_context(tc.tile_pool(name="reused", bufs=1))
        psum = ctx.enter_context(tc.psum_pool(name="psum", bufs=1))

        def new(name, shape, dtype, tag=None):
            return keep.tile(shape, dtype, name=name, tag=tag or name, align_bytes=64)

        def placed(name, shape, dtype, offset):
            return reused.tile(shape, dtype, name=name, offset=offset, align_bytes=64)

        def bank(index, name, shape):
            return psum.tile(shape, F32, name=name, tag="bank%d" % index)

        def load_list(name, src):
            tile = new(name, [P, S // 16], U16)
            nc.sync.dma_start(tile[:], src)
            return tile

        def load_scale_rows(tile, first_row, src):
            for r in range(PACK):
                nc.sync.dma_start(
                    out=tile[first_row + r : P : 32, :].bitcast(I32),
                    in_=src[0, r : 16 : 4, :].bitcast(I32),
                )

        def words_of(src):
            return src[0].rearrange("p n r -> p (n r)").bitcast(I32)

        def entries(tile, start, count):
            return tile[:, start // 16 : (start + count) // 16]

        def quantize(codes, scales, grouped):
            nc.vector.quantize_mx(out=codes.bitcast(FP8X4), scales=scales, in_=grouped)

        def mm(out, lhs_codes, lhs_scales, rhs_codes, rhs_scales, start=True, stop=True):
            nc.tensor.matmul_mx(
                out=out, lhsT=lhs_codes.bitcast(FP8X4), lhsT_scale=lhs_scales,
                rhs=rhs_codes.bitcast(FP8X4), rhs_scale=rhs_scales, start=start, stop=stop,
            )

        def as_words(grouped):
            return grouped.rearrange("p (c i t) -> p c t i", i=PAIR, t=PACK)

        def as_planes(planes):
            return planes.rearrange("p t (c i) -> p c t i", i=PAIR)

        xs = new("xs", [P, T], U8)
        nc.vector.memset(xs[:].bitcast(I32), 0)
        ws = new("ws", [P, N], U8)
        nc.gpsimd.memset(ws[:].bitcast(I32), 0)
        book_t = load_list("book_t", book)
        raw = {}

        def load_half(name, w, h):
            raw[name, h] = new("%s_raw%d" % (name, h), [P, PACK, HALF], F32)
            nc.sync.dma_start(
                out=raw[name, h][:],
                in_=w.rearrange("(p j) c -> p j c", j=PACK)[:, :, h * HALF : (h + 1) * HALF],
            )

        load_half("w2", w2, 0)
        offs_t = load_list("offs_t", offs)
        load_scale_rows(xs, 0, x_scales)
        load_half("w2", w2, 1)
        xw = new("xw", [P, T], I32)
        nc.sync.dma_start(out=xw[:], in_=words_of(x_words))
        c1_t = load_list("c1_t", c1)
        c2_t = load_list("c2_t", c2)
        load_half("w1", w1, 0)
        load_half("w1", w1, 1)
        load_scale_rows(ws, 0, w3_scales)
        load_scale_rows(ws, 4, w4_scales)
        ww = new("ww", [P, 2, N], I32)
        nc.sync.dma_start(out=ww[:, 0, :], in_=words_of(w3_words))
        nc.sync.dma_start(out=ww[:, 1, :], in_=words_of(w4_words))

        bs = new("bs", [P, V], U8)
        nc.vector.tensor_copy(bs[:], xs[:].indirect(book_t[:]))
        ps = new("ps", [P, S], U8)
        nc.vector.tensor_copy(ps[:], xs[:].indirect(offs_t[:]))

        def dealt_views(grouped, name, h):
            dst = grouped[:].rearrange("p (t m j) -> p m t j", t=PACK, j=PACK)[:, h * 64 : (h + 1) * 64]
            src = raw[name, h][:].rearrange("p j (m t) -> p m t j", t=PACK)
            return dst, src

        w2_bf = new("w2_bf", [P, H * PACK], BF16)
        nc.scalar.activation(*dealt_views(w2_bf, "w2", 0), COPY)
        dst, src = dealt_views(w2_bf, "w2", 1)
        nc.scalar.copy(dst[:, :SCALAR_SHARE], src[:, :SCALAR_SHARE])
        nc.gpsimd.tensor_copy(dst[:, SCALAR_SHARE:], src[:, SCALAR_SHARE:])
        w2_codes = new("w2_codes", [P, H], U32)
        w2_sc = new("w2_sc", [P, H], U8)
        quantize(w2_codes[:], w2_sc[:], w2_bf[:])
        bw = new("bw", [P, V], U32)
        for h in range(2):
            nc.vector.tensor_copy(
                bw[:, h * HALF : (h + 1) * HALF], xw[:].bitcast(U32).indirect(entries(book_t, h * HALF, HALF))
            )
        pw = new("pw", [P, S], U32)
        nc.vector.tensor_copy(pw[:], xw[:].bitcast(U32).indirect(offs_t[:]))
        c_parts = []
        for t in range(PACK):
            cols = slice(t * P, (t + 1) * P)
            spans = ((0, HALF, 7), (HALF, V, 0)) if t == 0 else ((0, V, t),)
            parts = []
            for lo, hi, b in spans:
                acc = bank(b, "c_acc%d_%d" % (t, lo), [P, hi - lo])
                mm(acc[:], w2_codes[:, cols], w2_sc[:, cols], bw[:, lo:hi], bs[:, lo:hi])
                parts.append((lo, hi, acc))
            c_parts.append(parts)

        windows = [new("window%d" % t, [P, V], F32) for t in range(PACK)]
        g1 = [new("g1_%d" % h, [P, PACK, HALF], F32) for h in range(2)]
        g2 = new("g2", [P, PACK, HALF], F32)

        def scalar_window(t):
            for lo, hi, acc in c_parts[t]:
                nc.scalar.activation(windows[t][:, lo:hi], acc[:], COPY, scale=-0.5)

        def first_lookup(t, h):
            nc.scalar.activation(g1[h][:, t, :], windows[t][:].indirect(entries(c1_t, h * HALF, HALF)), COPY, scale=2.0)

        def second_lookup_view(t, h):
            return windows[t][:].indirect(entries(c2_t, h * HALF, HALF))

        scalar_window(0)
        nc.vector.tensor_scalar(windows[1][:], c_parts[1][0][2][:], -0.5, None, MULT)
        first_lookup(0, 0)
        scalar_window(2)
        for t in range(2):
            nc.vector.tensor_copy(g2[:, t, :], second_lookup_view(t, 1))
        first_lookup(1, 0)
        scalar_window(3)
        first_lookup(2, 0)
        first_lookup(3, 0)

        w1_bf = placed("w1_bf", [P, H * PACK], BF16, 0)
        for h in range(2):
            nc.gpsimd.tensor_copy(*dealt_views(w1_bf, "w1", h))
        w1_codes = placed("w1_codes", [P, H], U32, 4096)
        w1_sc = new("w1_sc", [P, H], U8)
        quantize(w1_codes[:], w1_sc[:], w1_bf[:])
        y = []
        for q in range(QUADS):
            js = slice(q * QUARTER, (q + 1) * QUARTER)
            y.append(bank(4 + q, "y_acc%d" % q, [P, PACK, QUARTER]))
            for t in range(PACK):
                cols = slice(t * P, (t + 1) * P)
                mm(y[q][:, t, :], w1_codes[:, cols], w1_sc[:, cols], pw[:, js], ps[:, js])

        both_lookups = placed("both_lookups", [P, PACK, HALF], F32, 0)
        for t in range(PACK):
            nc.vector.tensor_tensor(both_lookups[:, t, :], second_lookup_view(t, 0), g1[0][:, t, :], ADD)
        for t in range(PACK):
            first_lookup(t, 1)
        for t in range(2, PACK):
            nc.scalar.activation(g2[:, t, :], second_lookup_view(t, 1), COPY)

        wsd = placed("wsd", [P, N], U8, 4096)
        nc.gpsimd.tensor_copy(
            wsd[:].rearrange("p (t m) -> p t m", t=PACK),
            ws[:].rearrange("p (m t) -> p t m", t=PACK),
        )
        wd_both = placed("wd_both", [P, 2, N], I32, 4096 + N)
        wd = [wd_both[:, w, :] for w in range(2)]
        nc.gpsimd.tensor_copy(
            wd_both[:].rearrange("p w (t c i) -> p w c t i", t=PACK, i=4),
            ww[:].rearrange("p w (c i t) -> p w c t i", t=PACK, i=4),
        )

        out_codes = new("out_codes", [P, S], I32)
        out_scales = new("out_scales", [P, S], U8)
        out_rows = out_0.rearrange("(p t) j -> p t j", t=PACK)
        out_words = words_of(out_1)
        out_bf = new("out_bf", [P, S * PACK], BF16)

        rz_bf = [new("rz_bf%d" % q, [P, 2, QUARTER * PACK], BF16) for q in range(2)]
        rz_codes = [placed("rz_codes%d" % q, [P, 2, QUARTER], U32, 12288 + 8192 * q) for q in range(2)]
        rz_bf.extend(placed("rz_bf%d" % q, [P, 2, QUARTER * PACK], BF16, 12288 + 2048 * (q - 2) - 1536) for q in range(2, QUADS))
        rz_codes.extend(new("rz_codes%d" % q, [P, 2, QUARTER], U32) for q in range(2, QUADS))
        rz_scales = [new("rz_scales%d" % q, [P, 2, QUARTER], U8) for q in range(QUADS)]

        def quantize_residuals(q, which):
            quantize(
                rz_codes[q][:, which, :].rearrange("p a n -> p (a n)"),
                rz_scales[q][:, which, :].rearrange("p a n -> p (a n)"),
                rz_bf[q][:, which, :].rearrange("p a n -> p (a n)"),
            )

        def quarter_of(tile, q):
            return tile[:, :, (q % 2) * QUARTER : (q % 2 + 1) * QUARTER]

        def woven_sum(q, which, left, right):
            nc.vector.tensor_tensor(as_words(rz_bf[q][:, which, :]), as_planes(left), as_planes(right), ADD)

        r1 = {}

        def first_residual(q):
            r1[q] = new("r1_%d" % q, [P, PACK, QUARTER], F32)
            nc.vector.tensor_tensor(r1[q][:], y[q][:], quarter_of(g1[1], q), ADD)

        def weave_first_residual(q, engine_copy):
            engine_copy(as_words(rz_bf[q][:, 0, :]), as_planes(r1[q][:]))

        def passes(acc, q, which, planes, start, stop):
            for n, t in enumerate(planes):
                cols = slice(t * P, (t + 1) * P)
                mm(
                    acc[:, n, :], wd[which][:, cols], wsd[4 * which : P, cols],
                    rz_codes[q][:, which, :], rz_scales[q][:, which, :],
                    start and n == 0, stop and n == len(planes) - 1,
                )

        def rounded(q):
            return out_bf[:, q * QUARTER * PACK : (q + 1) * QUARTER * PACK]

        res = {}
        both, only_r1, only_z = slice(0, 2), slice(0, 1), slice(1, 2)

        def product(q):
            quantize_residuals(q, both)
            acc = bank(q, "out_acc%d" % q, [P, PACK, QUARTER])
            passes(acc, q, 0, range(PACK), True, False)
            passes(acc, q, 1, range(PACK), False, True)
            res[q] = new("res%d" % q, [P, PACK, QUARTER], F32)
            nc.scalar.copy(res[q][:], acc[:])
            nc.sync.dma_start(out=out_rows[:, :, q * QUARTER : (q + 1) * QUARTER], in_=res[q][:])

        def planes(start, count):
            js = slice(start, start + count)
            quantize(out_codes[:, js], out_scales[:, js], out_bf[:, start * PACK : (start + count) * PACK])
            nc.sync.dma_start(out=out_words[:, js], in_=out_codes[:, js])

        woven_sum(0, 0, y[0][:], quarter_of(g1[0], 0))
        woven_sum(0, 1, y[0][:], quarter_of(both_lookups, 0))
        woven_sum(1, 0, y[1][:], quarter_of(g1[0], 1))
        product(0)
        woven_sum(1, 1, y[1][:], quarter_of(both_lookups, 1))
        first_residual(2)
        product(1)
        first_residual(LAST)
        weave_first_residual(2, nc.vector.tensor_copy)
        woven_sum(2, 1, r1[2][:], quarter_of(g2, 2))
        weave_first_residual(LAST, nc.vector.tensor_copy)
        nc.scalar.copy(as_words(rounded(0)), as_planes(res[0][:]))
        product(2)
        quantize_residuals(LAST, only_r1)
        woven_sum(LAST, 1, r1[LAST][:], quarter_of(g2, LAST))
        last_acc = [bank(3 + u, "last_acc%d" % u, [P, 2, QUARTER]) for u in range(2)]
        for u in range(2):
            passes(last_acc[u], LAST, 0, (2 * u, 2 * u + 1), True, False)
        quantize_residuals(LAST, only_z)
        for u in range(2):
            passes(last_acc[u], LAST, 1, (2 * u, 2 * u + 1), False, True)
        nc.vector.tensor_copy(as_words(rounded(1)), as_planes(res[1][:]))
        res_last = new("res_last", [P, PACK, QUARTER], F32)
        js = slice(LAST * QUARTER, S)
        dst = as_words(rounded(LAST))

        def round_last(u, engine_copy):
            engine_copy(dst[:, :, 2 * u : 2 * u + 2], as_planes(last_acc[u][:]))

        def store_last(u, engine_copy):
            engine_copy(res_last[:, 2 * u : 2 * u + 2, :], last_acc[u][:])
            nc.sync.dma_start(out=out_rows[:, 2 * u : 2 * u + 2, js], in_=res_last[:, 2 * u : 2 * u + 2, :])

        round_last(0, nc.scalar.copy)
        round_last(1, nc.vector.tensor_copy)
        planes(0, HALF)
        nc.vector.tensor_copy(as_words(rounded(2)), as_planes(res[2][:]))
        store_last(0, nc.scalar.copy)
        store_last(1, nc.scalar.copy)
        planes(HALF, HALF)
        for q in range(QUADS):
            queue = nc.sync if q % 2 else nc.scalar
            queue.dma_start(
                out=out_2[0, 4 * q : 4 * q + 4, :].bitcast(I32),
                in_=out_scales[32 * q : 32 * q + 4, :].bitcast(I32),
            )
